import numpy as np, ml_dtypes
CORES = [5,29,101,125,133,157,229,253]
N = 8
BF = ml_dtypes.bfloat16
def gentries(a):
    return np.ascontiguousarray(a.reshape(8, 16, -1).transpose(0, 2, 1)).reshape(8, -1)
def gtable(e):
    e = np.asarray(e); return np.ascontiguousarray(e.reshape(8, -1, 16).transpose(0, 2, 1)).reshape(128, -1).astype(np.int32)
V, VM, RO = 3072, 100, 3
H = V // 2
def toward(rng, share):
    c = int(share * H); a, b = 2 * rng.permutation(H), 2 * rng.permutation(H) + 1; e, o = 2 * rng.permutation(H), 2 * rng.permutation(H) + 1
    t = np.zeros(V, np.int64); t[a[:c]] = o[:c]; t[a[c:]] = e[c:]; t[b[:c]] = e[:c]; t[b[c:]] = o[c:]
    return t
def lean(rng, s):
    t = np.zeros(V, np.int64); k = 2 * np.arange(H // 2); e = 2 * rng.permutation(H)
    t[s * H + k] = (1 - s) * H + 1 + rng.permutation(k); t[(1 - s) * H + k] = e[:H // 2]
    t[1::2] = rng.permutation(np.concatenate([e[H // 2:], s * H + 1 + k]))
    return t
def put(u, a, b):
    i = int(np.argmax(u == b)); u[i] = u[a]; u[a] = b
def targets(rng):
    return np.stack([toward(rng, s) for s in rng.permutation(np.array([0.4, 0.5, 0.5, 0.6, 0.7, 0.8, 0.9, 1.0]))])
def points(rng):
    return np.floor((rng.integers(VM // 4, VM + 1, (N, 8, 16, 1)) + 1) * rng.random((N, 8, 16, V))).astype(np.int64)
def nudge(rng, x):
    for g in range(8):
        j = rng.permutation(V)[:V // 16]; r = rng.integers(0, N, V // 16); i = rng.integers(0, 16, V // 16)
        v = x[r, g, i, j]; x[r, g, i, j] = np.where(v < VM, v + 1, v - 1)
    return x
def pack(rng, x, t, top=False):
    d = {"z": np.ascontiguousarray(x.reshape(N, 128, V)).astype(np.float32).astype(BF)}
    d["wt"] = np.where(top, 7, rng.integers(0, 8, (N, 128, 1))).astype(np.float32).astype(BF)
    d["q"] = np.stack([gtable(t)] * N)
    return d
def setup_inputs(rng):
    return pack(rng, points(rng), targets(rng))
def setup_inputs_ties(rng):
    s = rng.integers(0, VM + 1, (N, 8, 16, 6)); k = rng.permutation(np.array([2, 2, 3, 3, 4, 4, 6, 6]))
    ix = rng.integers(0, k[:, None], (8, V))
    return pack(rng, nudge(rng, np.take_along_axis(s, ix[None, :, None, :], 3)), targets(rng))
def setup_inputs_corners(rng):
    x = np.repeat(VM * rng.integers(0, 2, (N, 8, 1, V)), 16, axis=2)
    return pack(rng, nudge(rng, x), targets(rng), True)
def setup_inputs_ends(rng):
    j = np.arange(V); x = points(rng); x[..., 0] = 0; x[..., 1] = VM; x[..., V - 1] = VM
    t = np.zeros((8, V), np.int64); o = rng.permutation(8)
    t[o[0]] = (j + 1) % V; t[o[1]] = (j - 1) % V; t[o[2]] = j ^ 1; t[o[3]] = np.where(j % 2 == 0, V - 1 - j, (j + H + 1) % V)
    u = j.copy(); s = rng.random(V) < 0.5
    for p in range(2):
        i = np.flatnonzero(s & (j % 2 == p)); u[i] = rng.permutation(i)
    t[o[4]] = u
    y = x[:, o[5]]; y[:] = y[:, :, 2:3].copy()
    a = 2 * int(rng.integers(0, H)); b = (a + 2 * int(rng.integers(2, H - 3)) + 1) % V
    y[:, :, a] = VM - y[:, :, a]; y[:, :, b] = y[:, :, a]
    u = toward(rng, 0.7); put(u, a, b); t[o[5]] = u
    y = x[:, o[6]]; u = toward(rng, 0.5); put(u, V - 1, 0); put(u, 0, V - 2)
    y[:, :, [0, V - 2]] = y[:, :, [V - 3]]; y[:, :, [1, V - 1]] = VM - y[:, :, [V - 3]]
    e = 2 * np.arange(H); e = e[u[e] % 2 == 1]; y[:, :, e] = y[:, :, e - 1]; t[o[6]] = u
    y = x[:, o[7]]; y[:] = y[:, :, 2:3].copy(); t[o[7]] = rng.permutation(V)
    return pack(rng, x, t)
def setup_inputs_crowd(rng):
    x = points(rng); t = np.zeros((8, V), np.int64); o = rng.permutation(8); ev = 2 * np.arange(H)
    for i in range(5): t[o[i]] = toward(rng, (1.0, 1.0, 0.95, 0.9, 0.9)[i])
    t[o[5], ev] = (ev + 2 * rng.integers(1, H - 2) + 1) % V; t[o[5], ev + 1] = 2 * rng.permutation(H)
    t[o[6]] = lean(rng, 0); t[o[7]] = lean(rng, 1)
    for g in range(8):
        m = ev[t[g, ev] % 2 == 1]; y = x[:, g]; y[:, :, m] = y[:, :, t[g, m]]
    return pack(rng, x, t)
def setup_inputs_spread(rng):
    x = (VM + 1) * np.exp2(-rng.integers(0, 6, (N, 8, 1, V)).astype(np.float64)) * rng.random((N, 8, 16, V))
    x = np.floor(x * (rng.random((N, 8, 16, 1)) > 0.0625)).astype(np.int64)
    return pack(rng, np.minimum(x, VM), np.stack([toward(rng, s) for s in 0.1 + 0.9 * rng.random(8)]))
def check_inputs(d):
    bad = []
    v = np.asarray(d["z"]).astype(np.float32)
    if not np.all((v >= 0) & (v <= VM) & (v == np.floor(v))): bad.append("z holds whole numbers of its range")
    k = np.asarray(d["wt"]).astype(np.float32)
    if not np.all((k >= 0) & (k <= 7) & (k == np.floor(k))): bad.append("wt holds whole numbers of its range")
    if np.any(d["q"] != d["q"][:1]): bad.append("q alike on all ranks")
    if any(np.any(np.sort(gentries(a), axis=1) != np.arange(V)) for a in d["q"]): bad.append("q is a permutation in each group")
    return bad
def dist(c, k):
    return np.add.reduce(k * np.abs(c), axis=(0, 2))
def reference(z, wt, q):
    x = z.astype(np.float32).astype(np.int32).reshape(N, 8, 16, V); t = gentries(q[0]).astype(np.int64); j = np.arange(V)
    k = wt.astype(np.float32).astype(np.int32).reshape(N, 8, 16, 1)
    for rnd in range(RO):
        left, right = np.roll(x, 1, axis=3), np.roll(x, -1, axis=3); ix = t[None, :, None, :]
        a = np.take_along_axis(x, ix, 3); b = np.take_along_axis(right, ix, 3)
        gain = dist(left - x, k) + dist(x - right, k) - dist(left - right, k) - dist(a - x, k) - dist(x - b, k) + dist(a - b, k)
        moves = ((gain > 0) & (j % 2 == rnd % 2) & (t % 2 != j % 2)).astype(np.int64)
        guest = np.zeros((8, V), np.int64); np.put_along_axis(guest, t, moves, 1)
        w = 1 - moves + guest; base = np.add.accumulate(w, axis=1) - w
        new = np.where(moves == 1, np.take_along_axis(base, t, 1) + 1, base)
        old = np.argsort(new, axis=1)
        x = np.take_along_axis(x, old[None, :, None, :], 3)
        t = np.take_along_axis(np.take_along_axis(new, t, 1), old, 1)
    return {"yz": x.reshape(N, 128, V).astype(np.float32).astype(BF), "yq": np.stack([t] * N).astype(np.float32)}

@@ -1,0 +1,598 @@
+from concourse.bass import DstId, RemoteDMATransfer
+from concourse.mybir import AluOpType, ActivationFunctionType
+
+A = AluOpType
+F = ActivationFunctionType
+NN = 1536
+NB = 96
+HB = 48
+OC = NN + 16
+XW = OC + NN + 16
+OFF = 22400
+RO = 3
+
+
+def _sb(w, d="bfloat16"):
+    return ("sbuf", [128, w], d)
+
+
+SCRATCH = {
+    "Z": _sb(2 * NN + 16), "X0": _sb(XW), "X1": _sb(XW), "XC": _sb(NN), "EB": _sb(NN + 16),
+    "T2": _sb(NN), "T3": _sb(NN), "TA": _sb(NN), "TB": _sb(NN), "TE": _sb(NN),
+    "M1": _sb(NN + 16), "STAT": _sb(NN), "K1": _sb(NN, "float32"), "K2": _sb(NN),
+    "W": _sb(2 * NN), "WS": _sb(2 * NN, "float32"), "WN": _sb(4 * NN), "NQ": _sb(XW),
+    "RXS": _sb(768, "uint16"), "RXF": _sb(768, "float32"), "E12": _sb(1536), "ONES": _sb(384), "OF": _sb(NB),
+    "SND": _sb(RO * NB, "uint16"),
+    "qi": _sb(200, "int32"), "qf": _sb(200, "float32"), "qa": _sb(200, "float32"), "qb": _sb(200, "float32"),
+    "wb": _sb(8), "C": _sb(64, "float32"), "CI": _sb(8, "int32"), "LT": _sb(24, "float32"), "RM": _sb(16, "float32"),
+    "RM8": _sb(16, "float32"), "J": _sb(144, "float32"), "J16": _sb(128, "float32"), "J8": _sb(128, "float32"),
+    "JJ": _sb(128, "float32"), "SEL": _sb(640, "float32"), "ZWP": _sb(8), "ZWN": _sb(8),
+    "ZA": _sb(144), "ZB": _sb(144), "ZC": _sb(144), "ZAC": _sb(144), "ZQ": _sb(144), "ZG": _sb(144),
+    "ZAB": _sb(144), "ZBC": _sb(144), "ZABC": _sb(144), "LK": _sb(192, "uint16"),
+    "BLK": _sb(128), "B8": _sb(128), "TRI": _sb(128), "IDN": _sb(128), "IDM": _sb(128), "N15": _sb(128), "DB": _sb(128),
+    "DA": _sb(128), "C3": _sb(8), "KF": _sb(3 * NB, "float32"), "KB": _sb(4 * NB),
+    "KI": _sb(192, "int32"), "OD": _sb(192, "int32"), "U": _sb(192, "float32"), "R2": _sb(192, "float32"),
+    "P1": _sb(192, "int32"), "P2": _sb(192, "int32"), "PH": _sb(192, "float32"), "O8": _sb(192, "float32"),
+    "LA": _sb(NB, "uint16"), "LR": _sb(NB, "uint16"), "LN": _sb(192, "uint16"), "LI": _sb(NB, "uint16"),
+    "LS": _sb(NB, "uint16"), "LB": _sb(NB, "uint16"), "LO": _sb(NB, "uint16"), "LC": _sb(NB, "uint16"),
+    "SB2": _sb(NB, "float32"), "DS2": _sb(NB, "float32"), "S2": _sb(NB, "float32"), "C32": _sb(NB, "float32"),
+    "mc": _sb(128), "mn": _sb(NB), "dd": _sb(NB), "inc": _sb(NB, "float32"), "base": _sb(NB, "float32"),
+    "hb": _sb(3 * NB), "lo": _sb(3 * NB), "QO": _sb(192, "float32"),
+    "RL": ("dram", [RO, 128, HB], "uint16"),
+    "RX0": ("dram", [16, 128, HB], "uint16"), "RX1": ("dram", [16, 128, HB], "uint16"), "RX2": ("dram", [16, 128, HB], "uint16"),
+}
+PSUM = ("pe0", "pe1", "pe2", "pe3", "pg", "pa", "pb", "pc")
+for _k in PSUM:
+    SCRATCH[_k] = ("psum", [128, 512], "float32")
+NDMA = 56
+SEMAPHORES = ["qv", "qs", "qp", "qg", "sent"] + ["rx%d" % t for t in range(RO)] + ["d%d" % k for k in range(NDMA)]
+
+
+def _bits(engines):
+    m = 0
+    for e in engines:
+        m |= 1 << e
+    return m
+
+
+def helpers(rank_core, T, topo):
+    far = [d for d in T.cores if d != rank_core and not topo.may_write(rank_core, d)]
+    near = [d for d in T.cores if d not in far]
+    free = [c for c in topo.cores_of(rank_core) if c not in T.cores]
+    out = []
+    for half, die in enumerate(sorted(set(topo.die(c) for c in free))):
+        mine = [c for c in free if topo.die(c) == die]
+        port = [c for c in mine if all(topo.may_write(c, d) for d in far)][0]
+        rest = [c for c in mine if c != port and all(topo.may_write(c, d) for d in near)][0]
+        out.append((port, half, far))
+        out.append((rest, half, near))
+    return out
+
+
+def helper_program(g, core, src, half, dests, T, topo):
+    rank = T.rank_of(src)
+    eng = [e for e in topo.engines(core, dests[0]) if all(e in topo.engines(core, d) for d in dests)]
+    for t in range(RO):
+        g.wait_ge(T.sem["rx%d" % t], 4)
+        tr = []
+        for k, d in enumerate(dests):
+            rid, pid = topo.addr(d, core)
+            tr.append(RemoteDMATransfer(dst_ids=[DstId(rid=rid, pnc=pid)], dma_engine_mask=_bits(eng[2 * k:2 * k + 2]),
+                                        remote_sem=T.sem["rx%d" % t], src=T.RL[t], dst=T["RX%d" % t][2 * rank + half]))
+        g.remote_dma_fused(tr, local_sem=T.sem.sent)
+    g.wait_ge(T.sem.sent, RO * 2 * len(dests))
+
+
+def rank_program(g, core, T, topo):
+    rank = T.rank_of(core)
+    if rank is None:
+        for src in T.cores:
+            if core in topo.cores_of(src):
+                for c, half, dests in helpers(src, T, topo):
+                    if c == core:
+                        helper_program(g, core, src, half, dests, T, topo)
+        return
+
+    Q = {"v": g.vector, "s": g.scalar, "p": g.tensor, "g": g, "y": g.sync}
+    cnt = {"v": 0, "s": 0, "p": 0, "g": 0}
+    seen = {k: {} for k in Q}
+    log = {}
+    nd = [0]
+
+    def wait(q, sem, val):
+        if seen[q].get(sem, 0) < val:
+            Q[q].wait_ge(T.sem[sem], val)
+            seen[q][sem] = val
+
+    def deps(q, rd, wr, tok):
+        need = {}
+        acc = [(r, False) for r in rd] + [(w, True) for w in wr]
+        for (name, a, b, tag), w in acc:
+            ps = name in PSUM
+            for (a2, b2, tag2, w2, tok2) in log.get(name, []):
+                if ps:
+                    hit = tok2[0] != tok[0] or (q != "p" and (w or w2))
+                else:
+                    hit = a < b2 and a2 < b and (w or w2) and (tag is None or tag2 is None or tag == tag2)
+                    hit = hit and not (q == "p" and tok2[0] == "qp")
+                if hit:
+                    need[tok2[0]] = max(need.get(tok2[0], 0), tok2[1])
+        for sem, val in need.items():
+            wait(q, sem, val)
+        for (name, a, b, tag), w in acc:
+            old = log.get(name, [])
+            if w and tag is None and name not in PSUM:
+                old = [e for e in old if not (a <= e[0] and e[1] <= b)]
+            log[name] = [e for e in old if not (e[4][0] == tok[0] and e[:4] == (a, b, tag, w))] + [(a, b, tag, w, tok)]
+
+    def R(name, a=0, b=None, step=1, rows=128):
+        t = T[name]
+        if b is None:
+            b = t.shape[1]
+        return (t[0:rows, a:b:step] if step != 1 else t[0:rows, a:b], (name, a, b, None))
+
+    def row(name, r, a=0, b=NN):
+        return (T[name][r::16, a:b], (name, a, b, r))
+
+    def X(win, off):
+        return (win[0].indirect(off[0]), win[1], off[1])
+
+    def run(q, fn, ins, outs, inc=True):
+        rd, wr = [], []
+        for x in ins:
+            if isinstance(x, tuple):
+                rd += list(x[1:])
+        for x in outs:
+            wr.append(x[1])
+            rd += list(x[2:])
+        tok = ("q" + q, cnt[q] + 1)
+        deps(q, rd, wr, tok)
+        call = fn()
+        if inc:
+            call.then_inc(T.sem["q" + q], 1)
+            cnt[q] += 1
+
+    def ap(x):
+        return x[0] if isinstance(x, tuple) else x
+
+    def cp(o, i):
+        run("v", lambda: g.vector.tensor_copy(o[0], i[0]), [i], [o])
+
+    def tt(o, a, b, op):
+        run("v", lambda: g.vector.tensor_tensor(o[0], a[0], b[0], op), [a, b], [o])
+
+    def ts(o, a, s1, op0, s2=None, op1=None):
+        if op1 is None:
+            run("v", lambda: g.vector.tensor_scalar(o[0], a[0], ap(s1), None, op0), [a, s1], [o])
+        else:
+            run("v", lambda: g.vector.tensor_scalar(o[0], a[0], ap(s1), ap(s2), op0, op1), [a, s1, s2], [o])
+
+    def ms(o, val):
+        run("v", lambda: g.vector.memset(o[0], val), [], [o])
+
+    def scan(o, d0, d1, init, op0, op1):
+        run("v", lambda: g.vector.tensor_tensor_scan(o[0], d0[0], d1[0], ap(init), op0, op1), [d0, d1, init], [o])
+
+    def act(o, i, scale=None, bias=None, fn=None):
+        kw = {}
+        if scale is not None:
+            kw["scale"] = ap(scale)
+        if bias is not None:
+            kw["bias"] = ap(bias)
+        if fn is None:
+            fn = F.Identity if isinstance(bias, tuple) else F.Copy
+        run("s", lambda: g.scalar.activation(o[0], i[0], fn, **kw), [i, scale, bias], [o])
+
+    def mv(q, o, i):
+        (cp if q == "v" else act)(o, i)
+
+    def mms(lst, first=True, last=True):
+        for k, (o, l, r) in enumerate(lst):
+            st, en = first and k == 0, last and k == len(lst) - 1
+            run("p", lambda: g.tensor.matmul(o[0], l[0], r[0], st, en), [l, r], [o], inc=(k == len(lst) - 1))
+
+    def iota(o, pat, base, cm, fl=True):
+        if fl:
+            run("g", lambda: g.iota(o[0], pat, base, cm, allow_small_or_imprecise_dtypes=True), [], [o])
+        else:
+            run("g", lambda: g.iota(o[0], pat, base, cm), [], [o])
+
+    def clear(name, n):
+        iota(R(name, 0, n), [[0, n]], 0, 0)
+
+    def dma(q, o, i):
+        sem = "d%d" % nd[0]
+        nd[0] += 1
+        deps(q, [i[1]] if i[1] else [], [o[1]] if o[1] else [], (sem, 16))
+        Q[q].dma_start(o[0], i[0]).then_inc(T.sem[sem], 16)
+
+    def zl(name, r):
+        return R(name, 15 - r, 143 - r)
+
+    def tile(ps, z, buf, a=0):
+        mms([(R(ps, 0, NB), zl(z, r), R(buf, a + r, a + NN, 16)) for r in range(16)])
+
+    def col(k):
+        return R("C", k, k + 1)
+
+    def lt(k):
+        return R("LT", k, k + 1)
+
+    def rm(k):
+        return R("RM", k, k + 1)
+
+    (cP, cR, cG, cT15, cW, cTQ, cU, cAL, cSC, cWC, cWB, cGI, cX, cY, cI0, cI1, cIN, cSB, cK3, cK) = range(20)
+    H2 = NN // 2
+
+    dma("s", R("qi", 0, 192), (T.q[:, :], None))
+    NZ = 4
+    ZC = 2 * NN // NZ
+    for k in range(NZ):
+        dma("y", R("Z", k * ZC, (k + 1) * ZC), (T.z[:, k * ZC:(k + 1) * ZC], None))
+    dma("y", R("wb", 0, 1), (T.wt[:], None))
+
+    iota(R("CI", 0, 1), [[1, 1]], 0, 1, fl=False)
+    iota(R("JJ"), [[64, 8], [2, 16]], 0, 0)
+    iota(R("J"), [[1, 144]], 0, 0)
+    iota(R("J16"), [[16, 8], [0, 16]], 0, 0)
+    iota(R("J8"), [[0, 16], [16, 8]], 0, 0)
+    clear("K1", NN)
+    clear("WS", NN)
+    clear("W", 2 * NN)
+
+    def frame(ps, a):
+        cp(R("KI", a, a + NB), R(ps, 0, NB))
+        ts(R("OD", a, a + NB), R("KI", a, a + NB), 1, A.bitwise_and)
+        ts(R("U", a, a + NB), R("OD", a, a + NB), float(2 * NN - 1), A.mult)
+        tt(R("R2", a, a + NB), R("U", a, a + NB), R(ps, 0, NB), A.add)
+
+    def cand_list():
+        frame("pc", NB)
+        ts(R("LA"), R("R2", NB, 192), 0.5, A.mult, float(NN), A.min)
+        ts(R("LR"), R("R2", NB, 192), 0.5, A.mult)
+
+    def term(buf, z, a, b, first=False, last=False):
+        mms(([(R("pg", 0, NB), R("IDN"), R("OF"))] if first else [])
+            + [(R("pg", 8 * c, 8 * c + 8), R(buf, 128 * c, 128 * c + 128), R(z)) for c in range(a // 128, b // 128)], first, last)
+
+    def relu(out, x, pos, neg):
+        for j in range(4):
+            a = 384 * j
+            mms([(R("pe%d" % j, 0, 384), R("IDN"), R(x, pos + a, pos + a + 384)), (R("pe%d" % j, 0, 384), R("IDM"), R(x, neg + a, neg + a + 384))])
+            act(R(out, a, a + 384), R("pe%d" % j, 0, 384), fn=F.Relu)
+
+    def ta(x, a, b):
+        tt(R("TA", a, b), X(R(x, 0, OC), R("LA", a // 16, b // 16)), R(x, OC + a, OC + b), A.min)
+
+    def tb(x, a, b, own):
+        tt(R("TB", a, b), X(R(x, OC, XW), R("LA", a // 16, b // 16)), own, A.max)
+
+    def te(q, a, b):
+        mv(q, R("TE", a, b), X(R("EB"), R("LA", a // 16, b // 16)))
+
+    def records():
+        ts(col(cK), col(cR), float(NB), A.mult)
+        ts(R("KI", 0, NB), R("J", 0, NB), col(cK), A.add)
+        ts(R("P1", 0, NB), R("KI", 0, NB), 4032, A.bitwise_and)
+        ts(R("P2", 0, NB), R("KI", 0, NB), 63, A.bitwise_and)
+        ts(R("KF", 0, NB), R("P1", 0, NB), float(NN), A.add)
+        ts(R("KF", NB, 2 * NB), R("P2", 0, NB), 16.0, A.add)
+        cp(R("KF", 2 * NB, 3 * NB), R("P1", 0, NB))
+        cp(R("KB", 3 * NB, 4 * NB), R("P2", 0, NB))
+        cp(R("KB", 0, 3 * NB), R("KF"))
+
+    def record_rows():
+        for r, k in ((6, 0), (7, 1), (12, 2)):
+            dma("y", row("K1", r), R("KF", k * NB, k * NB + NB))
+        for r, k in ((0, 2), (1, 3), (2, 0), (3, 1)):
+            dma("y", row("K2", r), R("KB", k * NB, k * NB + NB))
+        for r, k in ((8, 6), (9, 7), (13, 7)):
+            dma("y", row("K1", r), row("K1", k))
+
+    def matrices():
+        ts(R("LT", 0, 17), R("J", 0, 17), col(cR), A.is_gt)
+        ts(R("RM"), R("J", 0, 16), col(cR), A.is_equal)
+        ts(R("B8"), R("J8"), col(cG), A.is_equal)
+        ts(col(cU), lt(8), -2.0, A.mult, lt(11), A.add)
+        ts(R("CI", 3, 4), R("CI", 0, 1), 120, A.bitwise_and)
+        ts(col(cAL), col(cU), lt(2), A.add)
+        cp(col(cX), R("CI", 3, 4))
+        ts(R("DA"), R("J", 0, 128), col(cP), A.is_equal, col(cAL), A.mult)
+        ts(R("RM8", 0, 12), R("J", 0, 96, 8), col(cX), A.is_equal)
+        mms([(R("pb", 0, 128), R("B8"), R("DA"))])
+        ts(col(cSC), col(cU), lt(4), A.add)
+        ts(col(cGI), lt(11), lt(10), A.subtract, lt(14), A.add)
+        ts(R("DB"), R("J", 0, 128), col(cP), A.is_equal, lt(8), A.mult)
+        ts(col(cGI), col(cGI), lt(12), A.subtract)
+        ms(R("ONES"), 1.0)
+        ts(R("ZG"), R("J"), col(cT15), A.is_equal, col(cGI), A.mult)
+
+    def matrices2():
+        ts(R("BLK"), R("J16"), col(cG), A.is_equal)
+        ts(col(cWC), lt(6), lt(4), A.subtract)
+        ts(R("DA"), R("J", 0, 128), col(cP), A.is_le, -1.0, A.mult)
+        ts(col(cWB), col(cWC), -2.0, A.mult, lt(10), A.add)
+        ts(R("N15"), R("BLK"), rm(15), A.mult, -1.0, A.mult)
+        ts(col(cWB), col(cWB), lt(2), A.subtract)
+        ts(R("ZA"), R("J"), col(cT15), A.is_equal, lt(2), A.mult)
+        ts(R("ZC"), R("J"), col(cT15), A.is_equal, col(cWC), A.mult)
+        tt(R("TRI"), R("DA"), R("BLK"), A.mult)
+        ts(R("ZB"), R("J"), col(cT15), A.is_equal, col(cWB), A.mult)
+        ts(R("ZQ"), R("J"), col(cT15), A.is_equal, lt(4), A.mult)
+        tt(R("ZAC", 1, 144), R("ZA", 1, 144), R("ZC", 0, 143), A.add)
+        ts(R("C3", 0, 1), rm(0), float(2 * NN), A.mult)
+        ts(col(cI0), col(cR), 2.0, A.mult, -31.0, A.add)
+        ts(col(cI1), col(cR), 2.0, A.mult, -33.0, A.add)
+        ts(col(cK3), rm(3), float(2 * NN), A.mult)
+        ms(R("C32"), 32.0)
+        ts(R("M1", 0, 16), R("J", 0, 16), 0.0, A.mult, lt(4), A.add)
+        ms(R("X1", NN, OC), 0.0)
+        ms(R("X1", OC + NN, XW), 100.0)
+        ms(R("NQ", NN, OC), 0.0)
+        ts(col(cY), col(cR), 576.0, A.mult, 960.0, A.add)
+        ts(col(cSB), rm(15), float(2 - 576 * 16), A.mult, col(cY), A.add)
+        ts(R("SB2"), R("J", 0, NB), 2.0, A.mult, col(cSB), A.add)
+        ts(R("SB2", NB - 1, NB), rm(15), -192.0, A.mult, R("SB2", NB - 1, NB), A.add)
+
+    hs = helpers(core, T, topo)
+
+    def send(t):
+        s = R("SND", t * NB, (t + 1) * NB)
+        cp(s, R("pg", 0, NB))
+        deps("g", [s[1]], [], ("sent", 16 * (t + 1)))
+        tr = []
+        for k, (c, half, dests) in enumerate(hs):
+            rid, pid = topo.addr(c, core)
+            tr.append(RemoteDMATransfer(dst_ids=[DstId(rid=rid, pnc=pid)], dma_engine_mask=_bits(topo.engines(core, c)[4 * k:4 * k + 4]),
+                                        remote_sem=T.sem["rx%d" % t], src=T.SND[:, t * NB + half * HB:t * NB + (half + 1) * HB], dst=T.RL[t]))
+        g.remote_dma_fused(tr, local_sem=T.sem.sent)
+
+    def guests():
+        act(X(R("WS"), R("LR")), R("K1"), fn=F.Silu)
+        act(R("STAT"), R("WS", 0, NN))
+
+    def guests2():
+        tile("pb", "ZG", "STAT")
+        for r in range(6):
+            dma("s", row("STAT", r), row("K2", r if r < 4 else r - 2))
+
+    def new_lists():
+        frame("pa", 0)
+        ts(R("P1"), R("KI"), 1, A.logical_shift_right, 15, A.bitwise_and)
+        ts(R("P2"), R("KI"), 4, A.logical_shift_right, 4094, A.bitwise_and)
+        ts(R("O8"), R("R2"), float(4 * NN), A.add)
+        ts(R("PH"), R("P1"), 576.0, A.mult)
+        tt(R("O8"), R("O8"), R("OD"), A.mult)
+        tt(R("PH"), R("PH"), R("P2"), A.add)
+        tt(R("O8"), R("O8"), R("PH"), A.max)
+        tt(R("DS2"), R("PH", NB, 192), R("SB2"), A.subtract)
+        ts(R("LN"), R("O8"), 0.5, A.mult)
+        ts(R("DS2"), R("DS2"), 192.0, A.add)
+
+    def ones():
+        for j in range(4):
+            mms([(R("pe%d" % j, 0, 384), R("DB"), R("ONES"))], last=False)
+
+    def decide(t):
+        wait("y", "rx%d" % t, 4 * len(T.cores))
+        dma("y", R("RXS"), (T["RX%d" % t][:], None))
+        cp(R("LI"), R("pb", 0, NB))
+        for a, b in ((0, 2), (2, 5), (5, 8)):
+            cp(R("RXF", NB * a, NB * b), R("RXS", NB * a, NB * b))
+            mms([(R("pg", k, 128, 8, NB), R("RXF", NB * k, NB * k + NB), R("RM")) for k in range(a, b)], a == 0, b == 8)
+        ts(R("mc", rows=NB), R("pg", 0, 128, rows=NB), float(8 * OFF), A.is_gt)
+        for j in (0, 2, 1, 3):
+            lst = []
+            for c in range(3 * j, 3 * j + 3):
+                for e in (0, 1):
+                    x = 6 * e + c % 6
+                    lst.append((R("pe%d" % j, 128 * (c % 3) + e, 128 * (c % 3) + 128, 2), R("E12", 128 * x, 128 * x + 128, rows=NB),
+                                R("mc", 64 * (c // 6), 64 * (c // 6) + 64, rows=NB)))
+            mms(lst, first=False)
+
+        def m2(j):
+            tt(R("T2", 384 * j, 384 * j + 384), R("pe%d" % j, 0, 384), R("STAT", 384 * j, 384 * j + 384), A.mult)
+
+        for j in (0, 1):
+            act(R("M1", 16 + 384 * j, 400 + 384 * j), R("pe%d" % j, 0, 384), scale=col(cSC), bias=lt(8))
+        for j in (2, 3):
+            ts(R("M1", 16 + 384 * j, 400 + 384 * j), R("pe%d" % j, 0, 384), col(cSC), A.mult, lt(8), A.add)
+        tile("pa", "ZG", "M1", 16)
+        GS = 56
+        act(R("T3", 0, 16 * GS), X(R("M1"), R("LI", 0, GS)))
+        cp(R("T3", 16 * GS, NN), X(R("M1"), R("LI", GS, NB)))
+        tile("pb", "ZG", "T3")
+        cp(R("mn"), R("pa", 0, NB))
+        if t % 2 == 0:
+            mms([(R("pa", 128, 129), R("N15"), R("mn", NB - 1, NB))])
+        m2(0)
+        m2(1)
+        if t % 2 == 0:
+            ts(col(cIN), R("pa", 128, 129), col(cI0), A.add)
+        tt(R("dd"), R("pb", 0, NB), R("mn"), A.subtract)
+        mms([(R("pc", 0, NB), R("BLK"), R("dd"))])
+        mms([(R("pg", 0, NB), R("TRI"), R("dd"))] + ([(R("pg", 0, 1), R("IDN"), R("C3", 0, 1))] if t % 2 else []))
+        m2(2)
+        scan(R("inc"), R("pc", 0, NB), R("C32"), col(cI1 if t % 2 else cIN), A.add, A.add)
+        tt(R("S2"), R("mn"), R("DS2"), A.mult)
+        tt(R("base"), R("pg", 0, NB), R("inc"), A.add)
+        for k in range(3):
+            act(R("hb", k * NB, k * NB + NB), R("base"))
+        tt(R("S2"), R("S2"), R("SB2"), A.add)
+        tt(R("lo", 0, NB), R("base"), R("hb", 0, NB), A.subtract)
+        dma("y", row("WN", 0, 0, 3 * NN), R("hb"))
+        act(R("lo", NB, 2 * NB), R("lo", 0, NB), bias=1.0)
+        act(R("lo", 2 * NB, 3 * NB), R("lo", 0, NB), bias=-1.0)
+        dma("s", row("WN", 1, 0, 3 * NN), R("lo"))
+        cp(R("LB"), R("base"))
+        ts(R("LS"), R("S2"), 0.5, A.mult)
+        m2(3)
+        tt(X(R("W"), R("LB")), R("T3"), R("T2"), A.mult)
+        act(R("WN", 3 * NN, 4 * NN), X(R("WN", 0, 3 * NN), R("LS")))
+        act(R("NQ", OC, OC + NN), X(R("WN"), R("LN", NB, 192)))
+        NS = 32 if t < RO - 1 else 56
+        act(R("NQ", 0, 16 * NS), X(R("WN"), R("LN", 0, NS)))
+        cp(R("NQ", 16 * NS, NN), X(R("WN"), R("LN", NS, NB)))
+
+        def w(s, a, b, step):
+            return R("W", s + step * a, s + step * (b - 1) + 1, step)
+
+        def wrap(ps, z, s, step, n):
+            return [(R(ps, 1, NB), zl(z, 0), w(s, 0, NB - 1, step)), (R(ps, 0, 1), zl(z, 0), w(s, n - 1, n, step))]
+
+        if t == RO - 1:
+            z16 = ["ZABC"] * 14 + ["ZAB", "ZA"]
+            mms([(R("pa", 0, NB), zl(z16[r], r), w(r, 0, NB, 16)) for r in range(16)]
+                + wrap("pa", "ZC", 14, 16, 192) + wrap("pa", "ZBC", 15, 16, 192))
+            mms([(R("pb", 0, NB), zl(z16[r], r), w(r, NB, 192, 16)) for r in range(16)]
+                + [(R("pb", 0, NB), zl(z, 0), w(s, NB - 1, 191, 16)) for z, s in (("ZC", 14), ("ZBC", 15))])
+            return
+        mms([(R("pa", 0, NB), zl("ZAC" if r < 15 else "ZA", r), w(2 * r, 0, NB, 32)) for r in range(16)]
+            + [(R("pa", 0, NB), zl("ZB", r + 1), w(2 * r + 1, 0, NB, 32)) for r in range(15)]
+            + wrap("pa", "ZC", 30, 32, NB) + wrap("pa", "ZB", 31, 32, NB))
+        mms([(R("pb", 0, NB), zl("ZAC" if r < 15 else "ZA", r), w(2 * r + 1, 0, NB, 32)) for r in range(16)]
+            + [(R("pb", 0, NB), zl("ZB", r), w(2 * r, 0, NB, 32)) for r in range(16)] + wrap("pb", "ZC", 31, 32, NB))
+
+    ts(R("CI", 1, 2), R("CI", 0, 1), 15, A.bitwise_and)
+    cp(col(cP), R("CI", 0, 1))
+    cp(col(cR), R("CI", 1, 2))
+    ms(R("X0", NN + 1, OC), 0.0)
+    tt(col(cG), col(cP), col(cR), A.subtract)
+    ms(R("X0", OC + NN, XW), 100.0)
+    ts(col(cTQ), col(cG), 4.0, A.mult, col(cR), A.add)
+    ts(col(cT15), col(cG), 15.0, A.add)
+    sels = [(0, 1), (1, 1), (0, 2), (1, 2), (2, 2)]
+    for k in (2, 3, 4, 0, 1):
+        ts(R("SEL", 128 * k, 128 * k + 128), R("JJ"), col(cTQ), A.subtract, float(16 * sels[k][0] - sels[k][1]), A.is_equal)
+    ts(R("IDN"), R("J", 0, 128), col(cP), A.is_equal)
+    ts(R("IDM"), R("J", 0, 128), col(cP), A.is_equal, -1.0, A.mult)
+    ts(R("qa", 0, 192), R("qi", 0, 192), -1.0, A.add)
+    ts(R("qb", 0, 192), R("qi", 0, 192), 0.0, A.is_equal, float(2 * NN), A.mult)
+    ms(R("EB", NN, NN + 16), -100.0)
+    tt(R("qf", 0, 192), R("qa", 0, 192), R("qb", 0, 192), A.add)
+    ms(R("OF"), float(OFF))
+    cp(R("qf", 192, 193), R("qf", 0, 1))
+    mms([(R("pc", 0, NB), R("SEL", 128 * k, 128 * k + 128), R("qf", sels[k][0], sels[k][0] + 191, 2)) for k in (2, 3, 4)])
+    mms([(R("pa", 0, NB), R("SEL", 128 * k, 128 * k + 128), R("qf", sels[k][0], sels[k][0] + 191, 2)) for k in (0, 1)])
+    records()
+    cand_list()
+
+    PZ = ZC // 2
+    cp(R("X0", NN, NN + 1), R("Z", 1, 2))
+    cp(R("Z", 2 * NN, 2 * NN + 1), R("Z", 0, 1))
+    for k in range(NZ):
+        act(R("X0", k * PZ, (k + 1) * PZ), R("Z", k * ZC + 1, (k + 1) * ZC, 2))
+        a, b = max(k * PZ - 1, 0), (k + 1) * PZ - (1 if k < NZ - 1 else 0)
+        cp(R("X0", OC + a, OC + b), R("Z", 2 * a + 2, 2 * b + 1, 2))
+    record_rows()
+
+    relu("EB", "X0", OC, 0)
+    relu("T3", "X0", 1, 0)
+    cp(col(cW), R("wb", 0, 1))
+    ta("X0", 0, H2)
+    ts(R("ZWP"), R("J", 0, 128, 16), col(cG), A.is_equal, col(cW), A.mult)
+    ta("X0", H2, NN)
+    ts(R("ZWN"), R("ZWP"), -1.0, A.mult)
+    term("EB", "ZWP", 0, NN, first=True)
+    relu("T2", "X0", 1, OC)
+    term("T3", "ZWN", 0, NN)
+    term("TA", "ZWP", 0, NN)
+    tb("X0", 0, H2, R("Z", 2, 2 * H2 + 1, 2))
+    tb("X0", H2, NN, R("Z", 2 * H2 + 2, 2 * NN + 1, 2))
+    te("s", 0, 640)
+    term("T2", "ZWP", 0, NN)
+    term("TB", "ZWN", 0, NN)
+    te("v", 640, NN - 256)
+    term("TE", "ZWP", 0, NN - 256)
+    te("v", NN - 256, NN)
+    term("TE", "ZWP", NN - 256, NN, last=True)
+    guests()
+    send(0)
+    clear("WN", 3 * NN)
+    matrices()
+    for r in range(12):
+        act(R("E12", 128 * r, 128 * r + 128), R("pb", 0, 128), scale=R("RM8", r, r + 1))
+    ones()
+    guests2()
+    matrices2()
+    new_lists()
+
+    for t in range(RO):
+        xo, xn = "X%d" % (t % 2), "X%d" % ((t + 1) % 2)
+        decide(t)
+        NQ = R("NQ", 0, OC + NN)
+        if t < RO - 1:
+            cp(R("LO"), R("pa", 0, NB))
+            cp(R(xn, 0, H2), X(R(xo), R("LO", 0, HB)))
+            act(R(xn, H2, NN), X(R(xo), R("LO", HB, NB)))
+            cp(R("LC"), R("pb", 0, NB))
+            clear("WS", NN)
+            act(R("TE", H2, NN), X(NQ, R("LC", HB, NB)))
+            cp(R(xn, NN, NN + 1), R(xn, 0, 1))
+            cp(R("TE", 0, H2), X(NQ, R("LC", 0, HB)))
+            relu("T3", xn, 1, 0)
+            cp(R(xn, OC, OC + H2), X(R(xo), R("LC", 0, HB)))
+            dma("y", R("XC", 0, H2), R(xn, OC, OC + H2))
+            tile("pc", "ZQ", "TE")
+            cp(R(xn, OC + H2, OC + NN), X(R(xo), R("LC", HB, NB)))
+            dma("y", R("XC", H2, NN), R(xn, OC + H2, OC + NN))
+            cand_list()
+            relu("EB", xn, OC, 0)
+            term("T3", "ZWN", 0, NN, first=True)
+            ta(xn, 0, H2)
+            relu("T2", xn, 1, OC)
+            term("EB", "ZWP", 0, NN)
+            ta(xn, H2, NN)
+            term("T2", "ZWP", 0, NN)
+            term("TA", "ZWP", 0, NN)
+            te("s", 0, H2)
+            te("s", H2, NN)
+            tb(xn, 0, H2, R("XC", 0, H2))
+            term("TE", "ZWP", 0, H2)
+            term("TB", "ZWN", 0, H2)
+            tb(xn, H2, NN - 256, R("XC", H2, NN - 256))
+            term("TE", "ZWP", H2, NN)
+            term("TB", "ZWN", H2, NN - 256)
+            tb(xn, NN - 256, NN, R("XC", NN - 256, NN))
+            term("TB", "ZWN", NN - 256, NN, last=True)
+            guests()
+            send(t + 1)
+            clear("W", 2 * NN)
+            cp(R("M1", 16, 16 + NN), X(NQ, R("LO")))
+            tile("pa", "ZQ", "M1", 16)
+            ones()
+            guests2()
+            ts(R("WN", NB, NB + 1), R("WN", NB, NB + 1), col(cK3), A.subtract if t == 0 else A.add)
+            new_lists()
+            if t == RO - 2:
+                tt(R("ZAB", 1, 144), R("ZA", 1, 144), R("ZB", 0, 143), A.add)
+                tt(R("ZBC", 1, 144), R("ZB", 1, 144), R("ZC", 0, 143), A.add)
+                tt(R("ZABC", 2, 144), R("ZAB", 2, 144), R("ZC", 0, 142), A.add)
+        else:
+            def xs(q, a, b):
+                mv(q, R("Z", 16 * a, 16 * b), X(R(xo), R("LK", a, b)))
+                dma("y", (T.yz[:, 16 * a:16 * b], None), R("Z", 16 * a, 16 * b))
+
+            def qs(q, k):
+                a, b = HB * k, HB * k + HB
+                mv(q, R("WN", 16 * a, 16 * b), X(NQ, R("LK", a, b)))
+                mms([(R("pc", 0, 192), zl("ZQ", r), R("WN", 192 * r, 192 * r + 192)) for r in range(4 * k, 4 * k + 4)], k == 0, k == 3)
+
+            cp(R("LK", 0, NB), R("pa", 0, NB))
+            xs("v", 0, 32)
+            cp(R("LK", NB, 192), R("pb", 0, NB))
+            xs("v", 32, 80)
+            xs("s", 128, 192)
+            xs("v", 80, 128)
+            qs("s", 0)
+            qs("v", 2)
+            qs("s", 1)
+            qs("v", 3)
+            cp(R("QO"), R("pc", 0, 192))
+            dma("s", (T.yq[:, :], None), R("QO"))
+
+    for k in range(nd[0]):
+        wait("y", "d%d" % k, 16)
+    for q in cnt:
+        wait("y", "q" + q, cnt[q])
+    g.wait_ge(T.sem.sent, 16 * RO)

@@ -4,11 +4,13 @@ from concourse.mybir import AluOpType, ActivationFunctionType
 A = AluOpType
 F = ActivationFunctionType
 NN = 1536
+V = 2 * NN
 NB = 96
 HB = 48
-OC = NN + 16
-XW = OC + NN + 16
+XW = V + 32
+XP = 32
 OFF = 22400
+BIG = 4096.0
 RO = 3
 
 
@@ -17,34 +19,32 @@ def _sb(w, d="bfloat16"):
 
 
 SCRATCH = {
-    "Z": _sb(2 * NN + 16), "X0": _sb(XW), "X1": _sb(XW), "XC": _sb(NN), "EB": _sb(NN + 16),
-    "T2": _sb(NN), "T3": _sb(NN), "TA": _sb(NN), "TB": _sb(NN), "TE": _sb(NN),
-    "M1": _sb(NN + 16), "STAT": _sb(NN), "K1": _sb(NN, "float32"), "K2": _sb(NN),
-    "W": _sb(2 * NN), "WS": _sb(2 * NN, "float32"), "WN": _sb(4 * NN), "NQ": _sb(XW),
-    "RXS": _sb(768, "uint16"), "RXF": _sb(768, "float32"), "E12": _sb(1536), "ONES": _sb(384), "OF": _sb(NB),
-    "SND": _sb(RO * NB, "uint16"),
-    "qi": _sb(200, "int32"), "qf": _sb(200, "float32"), "qa": _sb(200, "float32"), "qb": _sb(200, "float32"),
+    "X0": _sb(XP + V + 16), "X1": _sb(XP + V + 16), "EB0": _sb(XW), "EB1": _sb(XW), "W": _sb(XW), "WS": _sb(V),
+    "ZR": _sb(NB), "XC": _sb(NN), "R2": _sb(NN), "R3": _sb(NN), "TA": _sb(NN), "TB": _sb(NN), "TE": _sb(NN),
+    "Y": _sb(NN + 16), "T2": _sb(NN + 16), "T3": _sb(NN), "K1": _sb(NN), "QC": _sb(NN), "QO": _sb(NN + 16),
+    "WN3": _sb(3 * NN + 16), "WN2": _sb(V), "WF3": _sb(3 * NN, "float32"), "WF2": _sb(V, "float32"), "QF": _sb(V, "float32"),
+    "RXS": _sb(768, "uint16"), "RXF": _sb(768, "float32"), "E12": _sb(1536), "OF": _sb(NB),
+    "SND": _sb(RO * NB, "uint16"), "TW": _sb(512, "float32"),
+    "qi": _sb(192, "int32"), "qf": _sb(192, "float32"), "qa": _sb(192, "int32"), "qb": _sb(192, "int32"), "qh": _sb(384),
     "wb": _sb(8), "C": _sb(64, "float32"), "CI": _sb(8, "int32"), "LT": _sb(24, "float32"), "RM": _sb(16, "float32"),
     "RM8": _sb(16, "float32"), "J": _sb(144, "float32"), "J16": _sb(128, "float32"), "J8": _sb(128, "float32"),
-    "JJ": _sb(128, "float32"), "SEL": _sb(640, "float32"), "ZWP": _sb(8), "ZWN": _sb(8),
-    "ZA": _sb(144), "ZB": _sb(144), "ZC": _sb(144), "ZAC": _sb(144), "ZQ": _sb(144), "ZG": _sb(144),
-    "ZAB": _sb(144), "ZBC": _sb(144), "ZABC": _sb(144), "LK": _sb(192, "uint16"),
-    "BLK": _sb(128), "B8": _sb(128), "TRI": _sb(128), "IDN": _sb(128), "IDM": _sb(128), "N15": _sb(128), "DB": _sb(128),
-    "DA": _sb(128), "C3": _sb(8), "KF": _sb(3 * NB, "float32"), "KB": _sb(4 * NB),
-    "KI": _sb(192, "int32"), "OD": _sb(192, "int32"), "U": _sb(192, "float32"), "R2": _sb(192, "float32"),
-    "P1": _sb(192, "int32"), "P2": _sb(192, "int32"), "PH": _sb(192, "float32"), "O8": _sb(192, "float32"),
-    "LA": _sb(NB, "uint16"), "LR": _sb(NB, "uint16"), "LN": _sb(192, "uint16"), "LI": _sb(NB, "uint16"),
-    "LS": _sb(NB, "uint16"), "LB": _sb(NB, "uint16"), "LO": _sb(NB, "uint16"), "LC": _sb(NB, "uint16"),
-    "SB2": _sb(NB, "float32"), "DS2": _sb(NB, "float32"), "S2": _sb(NB, "float32"), "C32": _sb(NB, "float32"),
-    "mc": _sb(128), "mn": _sb(NB), "dd": _sb(NB), "inc": _sb(NB, "float32"), "base": _sb(NB, "float32"),
-    "hb": _sb(3 * NB), "lo": _sb(3 * NB), "QO": _sb(192, "float32"),
+    "JJ": _sb(128, "float32"), "JM": _sb(128, "float32"), "JC": _sb(128, "float32"), "SEL": _sb(256, "float32"),
+    "ZWP": _sb(8), "ZWN": _sb(8), "ZQ": _sb(144), "ZG": _sb(144), "IDF": _sb(128, "float32"), "SELW": _sb(48),
+    "BLK": _sb(128), "B8": _sb(128), "TLT": _sb(128), "TGE": _sb(128), "IDN": _sb(128), "IDM": _sb(128), "DA": _sb(128),
+    "RS": _sb(128), "RC": _sb(128), "RQ": _sb(128), "KB": _sb(2 * NB),
+    "KI": _sb(NB, "int32"), "P1": _sb(NB, "int32"), "P2": _sb(NB, "int32"), "PA": _sb(NB, "float32"), "PB": _sb(NB, "float32"),
+    "LA": _sb(NB, "uint16"), "LA1": _sb(NB, "uint16"), "LI": _sb(NB, "uint16"), "LS": _sb(NB, "uint16"),
+    "LB": _sb(NB, "uint16"), "LSO": _sb(NB, "uint16"), "LX": _sb(2 * NB, "uint16"), "LQ": _sb(2 * NB, "uint16"),
+    "SB0": _sb(NB, "float32"), "SB1": _sb(NB, "float32"), "DS": _sb(NB, "float32"), "S2": _sb(NB, "float32"),
+    "C32": _sb(NB, "float32"), "mc": _sb(128), "mn": _sb(NB), "dd": _sb(NB), "base": _sb(NB, "float32"),
+    "hb": _sb(3 * NB), "lo": _sb(3 * NB), "b3": _sb(3 * NB, "float32"),
     "RL": ("dram", [RO, 128, HB], "uint16"),
     "RX0": ("dram", [16, 128, HB], "uint16"), "RX1": ("dram", [16, 128, HB], "uint16"), "RX2": ("dram", [16, 128, HB], "uint16"),
 }
 PSUM = ("pe0", "pe1", "pe2", "pe3", "pg", "pa", "pb", "pc")
 for _k in PSUM:
     SCRATCH[_k] = ("psum", [128, 512], "float32")
-NDMA = 56
+NDMA = 48
 SEMAPHORES = ["qv", "qs", "qp", "qg", "sent"] + ["rx%d" % t for t in range(RO)] + ["d%d" % k for k in range(NDMA)]
 
 
@@ -104,6 +104,9 @@ def rank_program(g, core, T, topo):
             Q[q].wait_ge(T.sem[sem], val)
             seen[q][sem] = val
 
+    def apart(x, y):
+        return x is not None and y is not None and x[0] == y[0] and x[1] != y[1]
+
     def deps(q, rd, wr, tok):
         need = {}
         acc = [(r, False) for r in rd] + [(w, True) for w in wr]
@@ -113,7 +116,7 @@ def rank_program(g, core, T, topo):
                 if ps:
                     hit = tok2[0] != tok[0] or (q != "p" and (w or w2))
                 else:
-                    hit = a < b2 and a2 < b and (w or w2) and (tag is None or tag2 is None or tag == tag2)
+                    hit = a < b2 and a2 < b and (w or w2) and not apart(tag, tag2)
                     hit = hit and not (q == "p" and tok2[0] == "qp")
                 if hit:
                     need[tok2[0]] = max(need.get(tok2[0], 0), tok2[1])
@@ -129,10 +132,14 @@ def rank_program(g, core, T, topo):
         t = T[name]
         if b is None:
             b = t.shape[1]
-        return (t[0:rows, a:b:step] if step != 1 else t[0:rows, a:b], (name, a, b, None))
+        tag = ("par", a % 2) if step % 2 == 0 else None
+        return (t[0:rows, a:b:step] if step != 1 else t[0:rows, a:b], (name, a, b, tag))
+
+    def S(name, a, n, step, rows=128):
+        return R(name, a, a + step * (n - 1) + 1, step, rows)
 
     def row(name, r, a=0, b=NN):
-        return (T[name][r::16, a:b], (name, a, b, r))
+        return (T[name][r::16, a:b], (name, a, b, ("row", r)))
 
     def X(win, off):
         return (win[0].indirect(off[0]), win[1], off[1])
@@ -186,6 +193,12 @@ def rank_program(g, core, T, topo):
     def mv(q, o, i):
         (cp if q == "v" else act)(o, i)
 
+    def rl(q, o, i, bias):
+        if q == "v":
+            ts(o, i, bias, A.add, 0.0, A.max)
+        else:
+            act(o, i, bias=bias, fn=F.Relu)
+
     def mms(lst, first=True, last=True):
         for k, (o, l, r) in enumerate(lst):
             st, en = first and k == 0, last and k == len(lst) - 1
@@ -197,8 +210,8 @@ def rank_program(g, core, T, topo):
         else:
             run("g", lambda: g.iota(o[0], pat, base, cm), [], [o])
 
-    def clear(name, n):
-        iota(R(name, 0, n), [[0, n]], 0, 0)
+    def fill(o, n, val=0):
+        iota(o, [[0, n]], val, 0)
 
     def dma(q, o, i):
         sem = "d%d" % nd[0]
@@ -209,8 +222,8 @@ def rank_program(g, core, T, topo):
     def zl(name, r):
         return R(name, 15 - r, 143 - r)
 
-    def tile(ps, z, buf, a=0):
-        mms([(R(ps, 0, NB), zl(z, r), R(buf, a + r, a + NN, 16)) for r in range(16)])
+    def tile(ps, z, buf, a=0, step=1):
+        mms([(R(ps, 0, NB), zl(z, r), S(buf, a + step * r, NB, 16 * step)) for r in range(16)])
 
     def col(k):
         return R("C", k, k + 1)
@@ -221,118 +234,85 @@ def rank_program(g, core, T, topo):
     def rm(k):
         return R("RM", k, k + 1)
 
-    (cP, cR, cG, cT15, cW, cTQ, cU, cAL, cSC, cWC, cWB, cGI, cX, cY, cI0, cI1, cIN, cSB, cK3, cK) = range(20)
+    (cP, cR, cG, cT15, cW, cTQ, cAL, cU, cX, cY, cI0, cI1, cSB, cK, cP2, cP6, c2, cSW, cY0, cY1, cT0, cT1, cH, cN) = range(24)
     H2 = NN // 2
+    CH = 384
 
-    dma("s", R("qi", 0, 192), (T.q[:, :], None))
-    NZ = 4
-    ZC = 2 * NN // NZ
-    for k in range(NZ):
-        dma("y", R("Z", k * ZC, (k + 1) * ZC), (T.z[:, k * ZC:(k + 1) * ZC], None))
-    dma("y", R("wb", 0, 1), (T.wt[:], None))
+    dma("s", R("qi"), (T.q[:, :], None))
+    for k in range(4):
+        dma("y", R("X0", XP + 2 * CH * k, XP + 2 * CH * (k + 1)), (T.z[:, 2 * CH * k:2 * CH * (k + 1)], None))
+    dma("s", R("X0", XP - 2, XP), (T.z[:, V - 2:V], None))
+    dma("s", R("wb", 0, 1), (T.wt[:], None))
+    dma("s", R("X0", XP + V, XP + V + 2), (T.z[:, 0:2], None))
 
     iota(R("CI", 0, 1), [[1, 1]], 0, 1, fl=False)
-    iota(R("JJ"), [[64, 8], [2, 16]], 0, 0)
     iota(R("J"), [[1, 144]], 0, 0)
+    iota(R("JJ"), [[64, 8], [2, 16]], 0, 0)
     iota(R("J16"), [[16, 8], [0, 16]], 0, 0)
     iota(R("J8"), [[0, 16], [16, 8]], 0, 0)
-    clear("K1", NN)
-    clear("WS", NN)
-    clear("W", 2 * NN)
+    iota(R("JM"), [[16, 8], [0, 4], [1, 4]], 0, 0)
+    iota(R("JC"), [[16, 8], [0, 2], [1, 8]], 0, 0)
+    fill(S("WS", 1, NN, 2), NN)
 
-    def frame(ps, a):
-        cp(R("KI", a, a + NB), R(ps, 0, NB))
-        ts(R("OD", a, a + NB), R("KI", a, a + NB), 1, A.bitwise_and)
-        ts(R("U", a, a + NB), R("OD", a, a + NB), float(2 * NN - 1), A.mult)
-        tt(R("R2", a, a + NB), R("U", a, a + NB), R(ps, 0, NB), A.add)
+    nbank = [0]
 
-    def cand_list():
-        frame("pc", NB)
-        ts(R("LA"), R("R2", NB, 192), 0.5, A.mult, float(NN), A.min)
-        ts(R("LR"), R("R2", NB, 192), 0.5, A.mult)
+    def relu(out, a, n, x, pos, neg, step=1):
+        ps = "pe%d" % (nbank[0] % 4)
+        nbank[0] += 1
+        mms([(R(ps, 0, n), R("IDN"), S(x, pos, n, 2)), (R(ps, 0, n), R("IDM"), S(x, neg, n, 2))])
+        act(S(out, a, n, step), R(ps, 0, n), fn=F.Relu)
 
-    def term(buf, z, a, b, first=False, last=False):
+    def relus(x, par, j):
+        c = XP + par + 2 * CH * j
+        relu("EB%d" % par, c - XP + 15, CH + (1 if j == 3 and par == 0 else 0), x, c, c - 1, 2)
+        relu("R2", CH * j, CH, x, c + 1, c)
+        relu("R3", CH * j, CH, x, c + 1, c - 1)
+
+    def term(buf, z, a, b, first=False, last=False, at=0, step=1):
         mms(([(R("pg", 0, NB), R("IDN"), R("OF"))] if first else [])
-            + [(R("pg", 8 * c, 8 * c + 8), R(buf, 128 * c, 128 * c + 128), R(z)) for c in range(a // 128, b // 128)], first, last)
+            + [(R("pg", 8 * c, 8 * c + 8), S(buf, at + step * 128 * c, 128, step), R(z)) for c in range(a // 128, b // 128)], first, last)
 
-    def relu(out, x, pos, neg):
-        for j in range(4):
-            a = 384 * j
-            mms([(R("pe%d" % j, 0, 384), R("IDN"), R(x, pos + a, pos + a + 384)), (R("pe%d" % j, 0, 384), R("IDM"), R(x, neg + a, neg + a + 384))])
-            act(R(out, a, a + 384), R("pe%d" % j, 0, 384), fn=F.Relu)
+    def terms(par, j, first=False):
+        term("EB%d" % par, "ZWP", CH * j, CH * j + CH, first=first, at=15 + par, step=2)
+        term("R2", "ZWP", CH * j, CH * j + CH)
+        term("R3", "ZWN", CH * j, CH * j + CH)
 
-    def ta(x, a, b):
-        tt(R("TA", a, b), X(R(x, 0, OC), R("LA", a // 16, b // 16)), R(x, OC + a, OC + b), A.min)
+    def ta(x, par, a, b):
+        tt(R("TA", a, b), X(R(x, XP, XP + V), R("LA", a // 16, b // 16)), R("XC", a, b), A.min)
 
-    def tb(x, a, b, own):
-        tt(R("TB", a, b), X(R(x, OC, XW), R("LA", a // 16, b // 16)), own, A.max)
+    def tb(x, par, a, b):
+        tt(R("TB", a, b), X(R(x, XP, XP + V + 1), R("LA1", a // 16, b // 16)), R("XC", a, b), A.max)
 
-    def te(q, a, b):
-        mv(q, R("TE", a, b), X(R("EB"), R("LA", a // 16, b // 16)))
+    def own(q, x, par, j):
+        o, i = R("XC", CH * j, CH * j + CH), S(x, XP + par + 2 * CH * j, CH, 2)
+        if q == "v":
+            cp(o, i)
+        else:
+            run("g", lambda: g.affine_select(o[0], i[0], [[0, CH]], A.is_ge, 0.0, 0, 0), [i], [o])
 
-    def records():
-        ts(col(cK), col(cR), float(NB), A.mult)
-        ts(R("KI", 0, NB), R("J", 0, NB), col(cK), A.add)
-        ts(R("P1", 0, NB), R("KI", 0, NB), 4032, A.bitwise_and)
-        ts(R("P2", 0, NB), R("KI", 0, NB), 63, A.bitwise_and)
-        ts(R("KF", 0, NB), R("P1", 0, NB), float(NN), A.add)
-        ts(R("KF", NB, 2 * NB), R("P2", 0, NB), 16.0, A.add)
-        cp(R("KF", 2 * NB, 3 * NB), R("P1", 0, NB))
-        cp(R("KB", 3 * NB, 4 * NB), R("P2", 0, NB))
-        cp(R("KB", 0, 3 * NB), R("KF"))
+    def te(q, par, a, b):
+        mv(q, R("TE", a, b), X(R("EB%d" % par, 16, 16 + V), R("LA", a // 16, b // 16)))
 
-    def record_rows():
-        for r, k in ((6, 0), (7, 1), (12, 2)):
-            dma("y", row("K1", r), R("KF", k * NB, k * NB + NB))
-        for r, k in ((0, 2), (1, 3), (2, 0), (3, 1)):
-            dma("y", row("K2", r), R("KB", k * NB, k * NB + NB))
-        for r, k in ((8, 6), (9, 7), (13, 7)):
-            dma("y", row("K1", r), row("K1", k))
+    def lists():
+        cp(R("LA"), R("pa", 0, NB))
+        ts(R("LA1"), R("pa", 0, NB), 1.0, A.add)
+        cp(R("KI"), R("pa", 0, NB))
 
-    def matrices():
-        ts(R("LT", 0, 17), R("J", 0, 17), col(cR), A.is_gt)
-        ts(R("RM"), R("J", 0, 16), col(cR), A.is_equal)
-        ts(R("B8"), R("J8"), col(cG), A.is_equal)
-        ts(col(cU), lt(8), -2.0, A.mult, lt(11), A.add)
-        ts(R("CI", 3, 4), R("CI", 0, 1), 120, A.bitwise_and)
-        ts(col(cAL), col(cU), lt(2), A.add)
-        cp(col(cX), R("CI", 3, 4))
-        ts(R("DA"), R("J", 0, 128), col(cP), A.is_equal, col(cAL), A.mult)
-        ts(R("RM8", 0, 12), R("J", 0, 96, 8), col(cX), A.is_equal)
-        mms([(R("pb", 0, 128), R("B8"), R("DA"))])
-        ts(col(cSC), col(cU), lt(4), A.add)
-        ts(col(cGI), lt(11), lt(10), A.subtract, lt(14), A.add)
-        ts(R("DB"), R("J", 0, 128), col(cP), A.is_equal, lt(8), A.mult)
-        ts(col(cGI), col(cGI), lt(12), A.subtract)
-        ms(R("ONES"), 1.0)
-        ts(R("ZG"), R("J"), col(cT15), A.is_equal, col(cGI), A.mult)
-
-    def matrices2():
-        ts(R("BLK"), R("J16"), col(cG), A.is_equal)
-        ts(col(cWC), lt(6), lt(4), A.subtract)
-        ts(R("DA"), R("J", 0, 128), col(cP), A.is_le, -1.0, A.mult)
-        ts(col(cWB), col(cWC), -2.0, A.mult, lt(10), A.add)
-        ts(R("N15"), R("BLK"), rm(15), A.mult, -1.0, A.mult)
-        ts(col(cWB), col(cWB), lt(2), A.subtract)
-        ts(R("ZA"), R("J"), col(cT15), A.is_equal, lt(2), A.mult)
-        ts(R("ZC"), R("J"), col(cT15), A.is_equal, col(cWC), A.mult)
-        tt(R("TRI"), R("DA"), R("BLK"), A.mult)
-        ts(R("ZB"), R("J"), col(cT15), A.is_equal, col(cWB), A.mult)
-        ts(R("ZQ"), R("J"), col(cT15), A.is_equal, lt(4), A.mult)
-        tt(R("ZAC", 1, 144), R("ZA", 1, 144), R("ZC", 0, 143), A.add)
-        ts(R("C3", 0, 1), rm(0), float(2 * NN), A.mult)
-        ts(col(cI0), col(cR), 2.0, A.mult, -31.0, A.add)
-        ts(col(cI1), col(cR), 2.0, A.mult, -33.0, A.add)
-        ts(col(cK3), rm(3), float(2 * NN), A.mult)
-        ms(R("C32"), 32.0)
-        ts(R("M1", 0, 16), R("J", 0, 16), 0.0, A.mult, lt(4), A.add)
-        ms(R("X1", NN, OC), 0.0)
-        ms(R("X1", OC + NN, XW), 100.0)
-        ms(R("NQ", NN, OC), 0.0)
-        ts(col(cY), col(cR), 576.0, A.mult, 960.0, A.add)
-        ts(col(cSB), rm(15), float(2 - 576 * 16), A.mult, col(cY), A.add)
-        ts(R("SB2"), R("J", 0, NB), 2.0, A.mult, col(cSB), A.add)
-        ts(R("SB2", NB - 1, NB), rm(15), -192.0, A.mult, R("SB2", NB - 1, NB), A.add)
+    def gathered(x, par):
+        ta(x, par, 0, H2)
+        tb(x, par, 0, H2)
+        ta(x, par, H2, NN)
+        te("s", par, 0, H2)
+        te("s", par, H2, NN)
+        term("TA", "ZWP", 0, H2)
+        term("TB", "ZWN", 0, H2)
+        term("TA", "ZWP", H2, NN)
+        term("TE", "ZWP", 0, H2)
+        tb(x, par, H2, NN - 256)
+        term("TB", "ZWN", H2, NN - 256)
+        term("TE", "ZWP", H2, NN)
+        tb(x, par, NN - 256, NN)
+        term("TB", "ZWN", NN - 256, NN, last=True)
 
     hs = helpers(core, T, topo)
 
@@ -347,33 +327,35 @@ def rank_program(g, core, T, topo):
                                         remote_sem=T.sem["rx%d" % t], src=T.SND[:, t * NB + half * HB:t * NB + (half + 1) * HB], dst=T.RL[t]))
         g.remote_dma_fused(tr, local_sem=T.sem.sent)
 
-    def guests():
-        act(X(R("WS"), R("LR")), R("K1"), fn=F.Silu)
-        act(R("STAT"), R("WS", 0, NN))
+    def guests(par):
+        cp(X(R("WS"), R("LA")), R("K1"))
 
-    def guests2():
-        tile("pb", "ZG", "STAT")
-        for r in range(6):
-            dma("s", row("STAT", r), row("K2", r if r < 4 else r - 2))
-
-    def new_lists():
-        frame("pa", 0)
+    def moves(par):
         ts(R("P1"), R("KI"), 1, A.logical_shift_right, 15, A.bitwise_and)
-        ts(R("P2"), R("KI"), 4, A.logical_shift_right, 4094, A.bitwise_and)
-        ts(R("O8"), R("R2"), float(4 * NN), A.add)
-        ts(R("PH"), R("P1"), 576.0, A.mult)
-        tt(R("O8"), R("O8"), R("OD"), A.mult)
-        tt(R("PH"), R("PH"), R("P2"), A.add)
-        tt(R("O8"), R("O8"), R("PH"), A.max)
-        tt(R("DS2"), R("PH", NB, 192), R("SB2"), A.subtract)
-        ts(R("LN"), R("O8"), 0.5, A.mult)
-        ts(R("DS2"), R("DS2"), 192.0, A.add)
+        ts(R("P2"), R("KI"), 5, A.logical_shift_right)
+        ts(R("PA"), R("P1"), 288.0, A.mult, float(NB), A.add)
+        tt(R("PB"), R("P2"), R("SB%d" % par), A.subtract)
+        tt(R("DS"), R("PA"), R("PB"), A.add)
 
-    def ones():
+    def records(t):
+        par = t % 2
         for j in range(4):
-            mms([(R("pe%d" % j, 0, 384), R("DB"), R("ONES"))], last=False)
+            ps = "pe%d" % j
+            lst = [(R(ps, 0, CH), R("RS"), R("K1", CH * j, CH * j + CH))]
+            if t == 0:
+                src = "TA" if j < 2 else "TB"
+                lst += [(S(ps, r // 2, HB, 8), R("RQ" if r % 2 else "RC"), R(src, NB * r + HB * (j % 2), NB * r + HB * (j % 2) + HB))
+                        for r in range(16)]
+            else:
+                lst += [(R(ps, 0, CH), R("RC"), R("QC", CH * j, CH * j + CH)),
+                        (R(ps, 0, CH), R("RQ"), R("QO", CH * j + par, CH * j + CH + par))]
+            mms(lst, last=False)
+        if par:
+            mms([(R("pc", 0, 1), R("RQ"), R("QO", 0, 1))])
+            act(R("T2", 15, 16), R("pc", 0, 1))
 
     def decide(t):
+        par = t % 2
         wait("y", "rx%d" % t, 4 * len(T.cores))
         dma("y", R("RXS"), (T["RX%d" % t][:], None))
         cp(R("LI"), R("pb", 0, NB))
@@ -389,207 +371,235 @@ def rank_program(g, core, T, topo):
                     lst.append((R("pe%d" % j, 128 * (c % 3) + e, 128 * (c % 3) + 128, 2), R("E12", 128 * x, 128 * x + 128, rows=NB),
                                 R("mc", 64 * (c // 6), 64 * (c // 6) + 64, rows=NB)))
             mms(lst, first=False)
-
-        def m2(j):
-            tt(R("T2", 384 * j, 384 * j + 384), R("pe%d" % j, 0, 384), R("STAT", 384 * j, 384 * j + 384), A.mult)
-
-        for j in (0, 1):
-            act(R("M1", 16 + 384 * j, 400 + 384 * j), R("pe%d" % j, 0, 384), scale=col(cSC), bias=lt(8))
-        for j in (2, 3):
-            ts(R("M1", 16 + 384 * j, 400 + 384 * j), R("pe%d" % j, 0, 384), col(cSC), A.mult, lt(8), A.add)
-        tile("pa", "ZG", "M1", 16)
-        GS = 56
-        act(R("T3", 0, 16 * GS), X(R("M1"), R("LI", 0, GS)))
-        cp(R("T3", 16 * GS, NN), X(R("M1"), R("LI", GS, NB)))
+        for j in range(4):
+            rl("s" if j < 2 else "v", R("Y", 16 + CH * j, 16 + CH * j + CH), R("pe%d" % j, 0, CH), col(cY0 + par))
+        tile("pa", "ZG", "Y", 16)
+        GS = 48
+        act(R("T3", 0, 16 * GS), X(R("Y"), R("LI", 0, GS)))
+        cp(R("T3", 16 * GS, NN), X(R("Y"), R("LI", GS, NB)))
         tile("pb", "ZG", "T3")
         cp(R("mn"), R("pa", 0, NB))
-        if t % 2 == 0:
-            mms([(R("pa", 128, 129), R("N15"), R("mn", NB - 1, NB))])
-        m2(0)
-        m2(1)
-        if t % 2 == 0:
-            ts(col(cIN), R("pa", 128, 129), col(cI0), A.add)
+        for j in range(3):
+            rl("s", R("T2", 16 + CH * j, 16 + CH * j + CH), R("pe%d" % j, 0, CH), col(cT0 + par))
+        rl("v", R("T2", 16 + CH * 3, 16 + NN), R("pe3", 0, CH), col(cT0 + par))
+        if par:
+            rl("v", R("W", 16 + V, 17 + V), R("pe3", CH - 1, CH), col(cT0 + par))
+        tt(R("S2"), R("mn"), R("DS"), A.mult)
         tt(R("dd"), R("pb", 0, NB), R("mn"), A.subtract)
-        mms([(R("pc", 0, NB), R("BLK"), R("dd"))])
-        mms([(R("pg", 0, NB), R("TRI"), R("dd"))] + ([(R("pg", 0, 1), R("IDN"), R("C3", 0, 1))] if t % 2 else []))
-        m2(2)
-        scan(R("inc"), R("pc", 0, NB), R("C32"), col(cI1 if t % 2 else cIN), A.add, A.add)
-        tt(R("S2"), R("mn"), R("DS2"), A.mult)
-        tt(R("base"), R("pg", 0, NB), R("inc"), A.add)
-        for k in range(3):
-            act(R("hb", k * NB, k * NB + NB), R("base"))
-        tt(R("S2"), R("S2"), R("SB2"), A.add)
-        tt(R("lo", 0, NB), R("base"), R("hb", 0, NB), A.subtract)
-        dma("y", row("WN", 0, 0, 3 * NN), R("hb"))
-        act(R("lo", NB, 2 * NB), R("lo", 0, NB), bias=1.0)
-        act(R("lo", 2 * NB, 3 * NB), R("lo", 0, NB), bias=-1.0)
-        dma("s", row("WN", 1, 0, 3 * NN), R("lo"))
+        mms([(R("pc", 0, NB), R("TLT"), R("dd")), (R("pc", 1, NB), R("TGE"), R("dd", 0, NB - 1))]
+            + ([] if par else [(R("pc", 0, NB), R("IDM"), R("mn")), (R("pc", 1, NB), R("IDN"), R("mn", 0, NB - 1))]))
+        tt(R("S2"), R("S2"), R("SB%d" % par), A.add)
+        scan(R("base"), R("pc", 0, NB), R("C32"), col(cI0 + par), A.add, A.add)
+        cp(R("LS"), R("S2"))
         cp(R("LB"), R("base"))
-        ts(R("LS"), R("S2"), 0.5, A.mult)
-        m2(3)
-        tt(X(R("W"), R("LB")), R("T3"), R("T2"), A.mult)
-        act(R("WN", 3 * NN, 4 * NN), X(R("WN", 0, 3 * NN), R("LS")))
-        act(R("NQ", OC, OC + NN), X(R("WN"), R("LN", NB, 192)))
-        NS = 32 if t < RO - 1 else 56
-        act(R("NQ", 0, 16 * NS), X(R("WN"), R("LN", 0, NS)))
-        cp(R("NQ", 16 * NS, NN), X(R("WN"), R("LN", NS, NB)))
+        tt(X(R("W", 16, 16 + V), R("LB")), R("T3"), R("T2", 16 - par, 16 - par + NN), A.add)
+        if t < RO - 1:
+            act(R("hb", 0, NB), R("base"), bias=col(cH), fn=F.Relu)
+            mms([(R("pa", 0, NB), R("IDF"), R("base")), (R("pa", 0, NB), R("IDM"), R("hb", 0, NB))])
+            for k in (1, 2):
+                act(R("hb", k * NB, k * NB + NB), R("hb", 0, NB))
+            dma("y", row("WN3", 0, 0, 3 * NN), R("hb"))
+            for k, d in enumerate((0.0, 1.0, -1.0)):
+                act(R("lo", k * NB, k * NB + NB), R("pa", 0, NB), bias=d)
+            dma("s", row("WN3", 1, 0, 3 * NN), R("lo"))
+            w3, w2 = "WN3", "WN2"
+        else:
+            for k, d in enumerate((0.0, 1.0, -1.0)):
+                act(R("b3", k * NB, k * NB + NB), R("base"), bias=d)
+            dma("s", row("WF3", 0, 0, 3 * NN), R("b3"))
+            w3, w2 = "WF3", "WF2"
+        act(S(w2, par, NN, 2), X(R(w3), R("LS")))
+        act(S(w2, 1 - par, NN, 2), X(R(w3), R("LSO")))
 
-        def w(s, a, b, step):
-            return R("W", s + step * a, s + step * (b - 1) + 1, step)
+        def w(s):
+            return S("W", 16 + s, NB, 32)
 
-        def wrap(ps, z, s, step, n):
-            return [(R(ps, 1, NB), zl(z, 0), w(s, 0, NB - 1, step)), (R(ps, 0, 1), zl(z, 0), w(s, n - 1, n, step))]
+        def pw(a, b):
+            return R("pg", a, b, rows=NB)
 
-        if t == RO - 1:
-            z16 = ["ZABC"] * 14 + ["ZAB", "ZA"]
-            mms([(R("pa", 0, NB), zl(z16[r], r), w(r, 0, NB, 16)) for r in range(16)]
-                + wrap("pa", "ZC", 14, 16, 192) + wrap("pa", "ZBC", 15, 16, 192))
-            mms([(R("pb", 0, NB), zl(z16[r], r), w(r, NB, 192, 16)) for r in range(16)]
-                + [(R("pb", 0, NB), zl(z, 0), w(s, NB - 1, 191, 16)) for z, s in (("ZC", 14), ("ZBC", 15))])
-            return
-        mms([(R("pa", 0, NB), zl("ZAC" if r < 15 else "ZA", r), w(2 * r, 0, NB, 32)) for r in range(16)]
-            + [(R("pa", 0, NB), zl("ZB", r + 1), w(2 * r + 1, 0, NB, 32)) for r in range(15)]
-            + wrap("pa", "ZC", 30, 32, NB) + wrap("pa", "ZB", 31, 32, NB))
-        mms([(R("pb", 0, NB), zl("ZAC" if r < 15 else "ZA", r), w(2 * r + 1, 0, NB, 32)) for r in range(16)]
-            + [(R("pb", 0, NB), zl("ZB", r), w(2 * r, 0, NB, 32)) for r in range(16)] + wrap("pb", "ZC", 31, 32, NB))
+        mms([(pw(0, 512), R("ZR"), R("K1", 0, 512))], last=False)
+        mms([(pw(16 * s - 16, 16 * s + 32), w(s), R("SELW")) for s in range(1, 31)]
+            + [(pw(0, 32), w(0), R("SELW", 16, 48)), (pw(480, 512), w(31), R("SELW", 0, 32)),
+               (pw(496, 512), w(32), R("SELW", 0, 16)), (pw(0, 16), w(-1), R("SELW", 32, 48))], first=False)
+        for k in range(8):
+            cp(R("TW", 64 * k, 64 * k + 64, rows=NB), S("pg", k, 64, 8, NB))
+
+    def turn(ps, a, par, f):
+        mms([(R(ps, a, a + NB), S("TW", 2 * par + f, 128, 4, NB), R("IDF", 0, NB, rows=NB))])
 
     ts(R("CI", 1, 2), R("CI", 0, 1), 15, A.bitwise_and)
     cp(col(cP), R("CI", 0, 1))
     cp(col(cR), R("CI", 1, 2))
-    ms(R("X0", NN + 1, OC), 0.0)
+    ms(S("EB0", 16, NN, 2), -200.0)
     tt(col(cG), col(cP), col(cR), A.subtract)
-    ms(R("X0", OC + NN, XW), 100.0)
-    ts(col(cTQ), col(cG), 4.0, A.mult, col(cR), A.add)
-    ts(col(cT15), col(cG), 15.0, A.add)
-    sels = [(0, 1), (1, 1), (0, 2), (1, 2), (2, 2)]
-    for k in (2, 3, 4, 0, 1):
-        ts(R("SEL", 128 * k, 128 * k + 128), R("JJ"), col(cTQ), A.subtract, float(16 * sels[k][0] - sels[k][1]), A.is_equal)
     ts(R("IDN"), R("J", 0, 128), col(cP), A.is_equal)
+    ts(col(cTQ), col(cG), 4.0, A.mult, col(cR), A.add)
     ts(R("IDM"), R("J", 0, 128), col(cP), A.is_equal, -1.0, A.mult)
-    ts(R("qa", 0, 192), R("qi", 0, 192), -1.0, A.add)
-    ts(R("qb", 0, 192), R("qi", 0, 192), 0.0, A.is_equal, float(2 * NN), A.mult)
-    ms(R("EB", NN, NN + 16), -100.0)
-    tt(R("qf", 0, 192), R("qa", 0, 192), R("qb", 0, 192), A.add)
+    for k in range(2):
+        ts(R("SEL", 128 * k, 128 * k + 128), R("JJ"), col(cTQ), A.subtract, float(16 * k), A.is_equal)
+    ts(col(cT15), col(cG), 15.0, A.add)
+    ts(col(cK), col(cR), float(NB), A.mult)
     ms(R("OF"), float(OFF))
-    cp(R("qf", 192, 193), R("qf", 0, 1))
-    mms([(R("pc", 0, NB), R("SEL", 128 * k, 128 * k + 128), R("qf", sels[k][0], sels[k][0] + 191, 2)) for k in (2, 3, 4)])
-    mms([(R("pa", 0, NB), R("SEL", 128 * k, 128 * k + 128), R("qf", sels[k][0], sels[k][0] + 191, 2)) for k in (0, 1)])
-    records()
-    cand_list()
-
-    PZ = ZC // 2
-    cp(R("X0", NN, NN + 1), R("Z", 1, 2))
-    cp(R("Z", 2 * NN, 2 * NN + 1), R("Z", 0, 1))
-    for k in range(NZ):
-        act(R("X0", k * PZ, (k + 1) * PZ), R("Z", k * ZC + 1, (k + 1) * ZC, 2))
-        a, b = max(k * PZ - 1, 0), (k + 1) * PZ - (1 if k < NZ - 1 else 0)
-        cp(R("X0", OC + a, OC + b), R("Z", 2 * a + 2, 2 * b + 1, 2))
-    record_rows()
-
-    relu("EB", "X0", OC, 0)
-    relu("T3", "X0", 1, 0)
+    cp(R("qf"), R("qi"))
+    mms([(R("pa", 0, NB), R("SEL", 128 * k, 128 * k + 128), S("qf", k, NB, 2)) for k in range(2)])
+    ts(R("P1"), R("J", 0, NB), col(cK), A.add)
+    ms(R("K1"), 0.0)
+    ts(R("P2"), R("P1"), 63, A.bitwise_and)
+    ts(R("P1"), R("P1"), 4032, A.bitwise_and)
+    ts(R("KB", NB, 2 * NB), R("P2"), 16.0, A.add)
+    cp(R("KB", 0, NB), R("P1"))
+    lists()
+    for k in range(2):
+        dma("y", row("K1", k), R("KB", k * NB, k * NB + NB))
     cp(col(cW), R("wb", 0, 1))
-    ta("X0", 0, H2)
+    ts(R("LT", 0, 17), R("J", 0, 17), col(cR), A.is_gt)
     ts(R("ZWP"), R("J", 0, 128, 16), col(cG), A.is_equal, col(cW), A.mult)
-    ta("X0", H2, NN)
+    ts(R("RM"), R("J", 0, 16), col(cR), A.is_equal)
     ts(R("ZWN"), R("ZWP"), -1.0, A.mult)
-    term("EB", "ZWP", 0, NN, first=True)
-    relu("T2", "X0", 1, OC)
-    term("T3", "ZWN", 0, NN)
-    term("TA", "ZWP", 0, NN)
-    tb("X0", 0, H2, R("Z", 2, 2 * H2 + 1, 2))
-    tb("X0", H2, NN, R("Z", 2 * H2 + 2, 2 * NN + 1, 2))
-    te("s", 0, 640)
-    term("T2", "ZWP", 0, NN)
-    term("TB", "ZWN", 0, NN)
-    te("v", 640, NN - 256)
-    term("TE", "ZWP", 0, NN - 256)
-    te("v", NN - 256, NN)
-    term("TE", "ZWP", NN - 256, NN, last=True)
-    guests()
+    ts(R("ZQ"), R("J"), col(cT15), A.is_equal, lt(2), A.mult)
+    ts(R("qa"), R("qi"), 4032, A.bitwise_and)
+    ts(R("qb"), R("qi"), 63, A.bitwise_and)
+    cp(R("qh", 0, 192), R("qa"))
+    cp(R("qh", 192, 384), R("qb"))
+
+    def matrices():
+        ts(R("B8"), R("J8"), col(cG), A.is_equal)
+        ts(col(cU), lt(12), lt(8), A.subtract, lt(4), A.subtract)
+        ts(R("CI", 3, 4), R("CI", 0, 1), 120, A.bitwise_and)
+        ts(col(cAL), col(cU), BIG, A.mult, rm(14), A.add)
+        cp(col(cX), R("CI", 3, 4))
+        ts(R("DA"), R("J", 0, 128), col(cP), A.is_equal, col(cAL), A.mult)
+        ts(R("RM8", 0, 12), R("J", 0, 96, 8), col(cX), A.is_equal)
+        mms([(R("pc", 0, 128), R("B8"), R("DA"))])
+        for r in range(12):
+            act(R("E12", 128 * r, 128 * r + 128), R("pc", 0, 128), scale=R("RM8", r, r + 1))
+        ts(col(c2), lt(2), 2.0, A.mult)
+        ts(col(cP2), col(cP), 2.0, A.add)
+        ts(col(cP6), col(cP), 6.0, A.add)
+        ts(R("RS"), R("JM"), col(cP), A.is_equal, col(c2), A.mult)
+        ts(R("RC"), R("JC"), col(cP2), A.is_equal, lt(2), A.mult)
+        ts(R("RQ"), R("J", 0, 128), col(cP6), A.is_equal, lt(2), A.mult)
+
+    def matrices2():
+        ts(R("ZG"), R("J"), col(cT15), A.is_equal, rm(14), A.mult)
+        ts(R("BLK"), R("J16"), col(cG), A.is_equal)
+        ts(R("DA"), R("J", 0, 128), col(cP), A.is_gt)
+        ts(R("IDF"), R("J", 0, 128), col(cP), A.is_equal)
+        tt(R("TLT"), R("DA"), R("BLK"), A.mult)
+        ts(R("CI", 4, 5), R("CI", 0, 1), 14, A.bitwise_and)
+        ts(col(cU), lt(12), lt(8), A.subtract, rm(14), A.add)
+        tt(R("TGE"), R("BLK"), R("TLT"), A.subtract)
+        ts(col(cSW), R("CI", 4, 5), 4.0, A.mult)
+        ts(col(cY), col(cU), -1.0, A.add, 65536.0, A.mult)
+        ts(col(cX), col(cG), 0.0625, A.mult, col(cSW), A.add)
+        ts(col(cU), lt(12), lt(8), A.subtract, -BIG, A.mult)
+        ts(col(cN), lt(8), -1.0, A.add, 65536.0, A.mult)
+        ts(R("SELW"), R("J", 0, 48), col(cX), A.is_equal)
+        ts(col(cY), col(cY), col(cU), A.add)
+        ts(col(cN), rm(5), col(cN), A.add)
+        tt(col(cU), rm(1), rm(5), A.add)
+        for par in range(2):
+            ts(col(cY0 + par), rm(9), float(par - 32), A.mult, col(cY), A.add)
+            ts(col(cT0 + par), col(cU), float(par - 32), A.mult, col(cN), A.add)
+            ts(col(cI0 + par), col(cR), 2.0, A.mult, float(-31 - par), A.add)
+        ms(R("C32"), 32.0)
+        ms(R("ZR"), 0.0)
+        ms(col(cH), -12.0)
+        ms(R("Y", 0, 16), 0.0)
+        ms(R("QO", NN, NN + 16), 0.0)
+        ts(col(cSB), col(cR), 288.0, A.mult)
+        ts(R("LSO"), R("J", 0, NB), col(cSB), A.add)
+        ts(R("SB0"), R("J", 0, NB), col(cSB), A.add, 192.0, A.add)
+        ts(col(cY), rm(15), float(1 - 288 * 16), A.mult, col(cSB), A.add)
+        ts(R("SB1"), R("J", 0, NB), col(cY), A.add, 480.0, A.add)
+        ts(R("SB1", NB - 1, NB), rm(15), float(3 * NN - 288), A.mult, R("SB1", NB - 1, NB), A.add)
+        ts(col(cY), rm(0), 3008.0, A.mult)
+        ts(col(cU), rm(1), 63.0, A.mult, col(cY), A.add)
+        ts(R("WN3", 3 * NN, 3 * NN + 16), R("C32", 0, 16), 0.0, A.mult, col(cU), A.add)
+
+    for j in range(4):
+        own("v", "X0", 0, j)
+        relus("X0", 0, j)
+        if j:
+            terms(0, j - 1, first=(j == 1))
+    terms(0, 3)
+    gathered("X0", 0)
     send(0)
-    clear("WN", 3 * NN)
+    fill(R("W"), XW)
+    fill(R("WN3", 0, 3 * NN), 3 * NN)
+    fill(S("EB1", 17, NN, 2), NN, -200)
+    for k, (buf, a) in enumerate((("TA", 0), ("TB", NB))):
+        for f in range(2):
+            dma("y", row(buf, f), R("qh", 192 * f + a, 192 * f + a + NB))
     matrices()
-    for r in range(12):
-        act(R("E12", 128 * r, 128 * r + 128), R("pb", 0, 128), scale=R("RM8", r, r + 1))
-    ones()
-    guests2()
+    guests(0)
+    records(0)
+    tile("pb", "ZQ", "WS", 1, 2)
     matrices2()
-    new_lists()
+    moves(0)
 
     for t in range(RO):
         xo, xn = "X%d" % (t % 2), "X%d" % ((t + 1) % 2)
+        par = (t + 1) % 2
+        win = R(xo, XP, XP + V)
         decide(t)
-        NQ = R("NQ", 0, OC + NN)
         if t < RO - 1:
-            cp(R("LO"), R("pa", 0, NB))
-            cp(R(xn, 0, H2), X(R(xo), R("LO", 0, HB)))
-            act(R(xn, H2, NN), X(R(xo), R("LO", HB, NB)))
-            cp(R("LC"), R("pb", 0, NB))
-            clear("WS", NN)
-            act(R("TE", H2, NN), X(NQ, R("LC", HB, NB)))
-            cp(R(xn, NN, NN + 1), R(xn, 0, 1))
-            cp(R("TE", 0, H2), X(NQ, R("LC", 0, HB)))
-            relu("T3", xn, 1, 0)
-            cp(R(xn, OC, OC + H2), X(R(xo), R("LC", 0, HB)))
-            dma("y", R("XC", 0, H2), R(xn, OC, OC + H2))
-            tile("pc", "ZQ", "TE")
-            cp(R(xn, OC + H2, OC + NN), X(R(xo), R("LC", HB, NB)))
-            dma("y", R("XC", H2, NN), R(xn, OC + H2, OC + NN))
-            cand_list()
-            relu("EB", xn, OC, 0)
-            term("T3", "ZWN", 0, NN, first=True)
-            ta(xn, 0, H2)
-            relu("T2", xn, 1, OC)
-            term("EB", "ZWP", 0, NN)
-            ta(xn, H2, NN)
-            term("T2", "ZWP", 0, NN)
-            term("TA", "ZWP", 0, NN)
-            te("s", 0, H2)
-            te("s", H2, NN)
-            tb(xn, 0, H2, R("XC", 0, H2))
-            term("TE", "ZWP", 0, H2)
-            term("TB", "ZWN", 0, H2)
-            tb(xn, H2, NN - 256, R("XC", H2, NN - 256))
-            term("TE", "ZWP", H2, NN)
-            term("TB", "ZWN", H2, NN - 256)
-            tb(xn, NN - 256, NN, R("XC", NN - 256, NN))
-            term("TB", "ZWN", NN - 256, NN, last=True)
-            guests()
+            fill(S("WS", 1 - par, NN, 2), NN)
+            turn("pa", 0, par, 1)
+            turn("pb", 0, 0, 0)
+            turn("pb", NB, 1, 0)
+            turn("pc", 0, 1 - par, 1)
+            cp(R("LQ", 0, NB), R("pa", 0, NB))
+            cp(R("LX"), R("pb", 0, 2 * NB))
+            act(R("QC"), X(R("WN2"), R("LQ", 0, NB)))
+            if par == 0:
+                cp(R(xn, 0, XP), X(win, R("LX", 2 * NB - 2, 2 * NB)))
+
+            def xs(j):
+                for e in range(2):
+                    cp(S(xn, XP + e + 2 * CH * j, CH, 2), X(win, R("LX", NB * e + 24 * j, NB * e + 24 * j + 24)))
+                own("g", xn, par, j)
+                if j == 0:
+                    cp(R(xn, XP + V, XP + V + 1), R(xn, XP, XP + 1))
+
+            xs(0)
+            cp(R("LQ", NB, 2 * NB), R("pc", 0, NB))
+            xs(1)
+            relus(xn, par, 0)
+            tile("pa", "ZQ", "QC")
+            xs(2)
+            relus(xn, par, 1)
+            lists()
+            xs(3)
+            relus(xn, par, 2)
+            relus(xn, par, 3)
+            for j in range(4):
+                terms(par, j, first=(j == 0))
+            gathered(xn, par)
             send(t + 1)
-            clear("W", 2 * NN)
-            cp(R("M1", 16, 16 + NN), X(NQ, R("LO")))
-            tile("pa", "ZQ", "M1", 16)
-            ones()
-            guests2()
-            ts(R("WN", NB, NB + 1), R("WN", NB, NB + 1), col(cK3), A.subtract if t == 0 else A.add)
-            new_lists()
-            if t == RO - 2:
-                tt(R("ZAB", 1, 144), R("ZA", 1, 144), R("ZB", 0, 143), A.add)
-                tt(R("ZBC", 1, 144), R("ZB", 1, 144), R("ZC", 0, 143), A.add)
-                tt(R("ZABC", 2, 144), R("ZAB", 2, 144), R("ZC", 0, 142), A.add)
+            fill(R("W"), XW)
+            if t == 0:
+                fill(R("WF3"), 3 * NN)
+            act(R("QO", 0, NN), X(R("WN2"), R("LQ", NB, 2 * NB)))
+            guests(par)
+            records(t + 1)
+            tile("pb", "ZQ", "WS", 1 - par, 2)
+            moves(par)
         else:
-            def xs(q, a, b):
-                mv(q, R("Z", 16 * a, 16 * b), X(R(xo), R("LK", a, b)))
-                dma("y", (T.yz[:, 16 * a:16 * b], None), R("Z", 16 * a, 16 * b))
-
-            def qs(q, k):
-                a, b = HB * k, HB * k + HB
-                mv(q, R("WN", 16 * a, 16 * b), X(NQ, R("LK", a, b)))
-                mms([(R("pc", 0, 192), zl("ZQ", r), R("WN", 192 * r, 192 * r + 192)) for r in range(4 * k, 4 * k + 4)], k == 0, k == 3)
-
-            cp(R("LK", 0, NB), R("pa", 0, NB))
-            xs("v", 0, 32)
-            cp(R("LK", NB, 192), R("pb", 0, NB))
-            xs("v", 32, 80)
-            xs("s", 128, 192)
-            xs("v", 80, 128)
-            qs("s", 0)
-            qs("v", 2)
-            qs("s", 1)
-            qs("v", 3)
-            cp(R("QO"), R("pc", 0, 192))
-            dma("s", (T.yq[:, :], None), R("QO"))
+            turn("pa", 0, 0, 0)
+            turn("pa", NB, 1, 0)
+            turn("pb", 0, 0, 1)
+            turn("pb", NB, 1, 1)
+            cp(R("LX"), R("pa", 0, 2 * NB))
+            cp(R("LQ"), R("pb", 0, 2 * NB))
+            for j in range(4):
+                for e, q in enumerate("vs"):
+                    mv(q, S(xn, XP + e + 2 * CH * j, CH, 2), X(win, R("LX", NB * e + 24 * j, NB * e + 24 * j + 24)))
+                dma("y", (T.yz[:, 2 * CH * j:2 * CH * (j + 1)], None), R(xn, XP + 2 * CH * j, XP + 2 * CH * (j + 1)))
+            for j in range(2):
+                for e, q in enumerate("vs"):
+                    mv(q, S("QF", e + NN * j, H2, 2), X(R("WF2"), R("LQ", NB * e + HB * j, NB * e + HB * j + HB)))
+                dma("y", (T.yq[:, NN * j:NN * (j + 1)], None), row("QF", 0, NN * j, NN * (j + 1)))
 
     for k in range(nd[0]):
         wait("y", "d%d" % k, 16)

@@ -7,6 +7,7 @@ NN = 1536
 V = 2 * NN
 NB = 96
 HB = 48
+QB = 24
 XW = V + 32
 XP = 32
 OFF = 22400
@@ -19,10 +20,11 @@ def _sb(w, d="bfloat16"):
 
 
 SCRATCH = {
-    "X0": _sb(XP + V + 16), "X1": _sb(XP + V + 16), "EB0": _sb(XW), "EB1": _sb(XW), "W": _sb(XW), "WS": _sb(V),
+    "X0": _sb(XP + V + 16), "X1": _sb(XP + V + 16), "EB0": _sb(XW), "EB1": _sb(XW), "W": _sb(XW),
+    "WS": _sb(3 * NN, "float32"), "WB": _sb(V), "K0": _sb(NN, "float32"), "ST": _sb(NN),
     "ZR": _sb(NB), "XC": _sb(NN), "R2": _sb(NN), "R3": _sb(NN), "TA": _sb(NN), "TB": _sb(NN), "TE": _sb(NN),
     "Y": _sb(NN + 16), "T2": _sb(NN + 16), "T3": _sb(NN), "K1": _sb(NN), "QC": _sb(NN), "QO": _sb(NN + 16),
-    "WN3": _sb(3 * NN + 16), "WN2": _sb(V), "WF3": _sb(3 * NN, "float32"), "WF2": _sb(V, "float32"), "QF": _sb(V, "float32"),
+    "WN3": _sb(3 * NN + 16), "WN2": _sb(V), "WF2": _sb(V, "float32"), "QF": _sb(V, "float32"),
     "RXS": _sb(768, "uint16"), "RXF": _sb(768, "float32"), "E12": _sb(1536), "OF": _sb(NB),
     "SND": _sb(RO * NB, "uint16"), "TW": _sb(512, "float32"),
     "qi": _sb(192, "int32"), "qf": _sb(192, "float32"), "qa": _sb(192, "int32"), "qb": _sb(192, "int32"), "qh": _sb(384),
@@ -31,7 +33,7 @@ SCRATCH = {
     "JJ": _sb(128, "float32"), "JM": _sb(128, "float32"), "JC": _sb(128, "float32"), "SEL": _sb(256, "float32"),
     "ZWP": _sb(8), "ZWN": _sb(8), "ZQ": _sb(144), "ZG": _sb(144), "IDF": _sb(128, "float32"), "SELW": _sb(48),
     "BLK": _sb(128), "B8": _sb(128), "TLT": _sb(128), "TGE": _sb(128), "IDN": _sb(128), "IDM": _sb(128), "DA": _sb(128),
-    "RS": _sb(128), "RC": _sb(128), "RQ": _sb(128), "KB": _sb(2 * NB),
+    "RS": _sb(128), "RC": _sb(128), "RQ": _sb(128), "RC0": _sb(128), "RQ0": _sb(128), "KQ": _sb(V), "KB": _sb(2 * NB, "float32"),
     "KI": _sb(NB, "int32"), "P1": _sb(NB, "int32"), "P2": _sb(NB, "int32"), "PA": _sb(NB, "float32"), "PB": _sb(NB, "float32"),
     "LA": _sb(NB, "uint16"), "LA1": _sb(NB, "uint16"), "LI": _sb(NB, "uint16"), "LS": _sb(NB, "uint16"),
     "LB": _sb(NB, "uint16"), "LSO": _sb(NB, "uint16"), "LX": _sb(2 * NB, "uint16"), "LQ": _sb(2 * NB, "uint16"),
@@ -39,13 +41,14 @@ SCRATCH = {
     "C32": _sb(NB, "float32"), "mc": _sb(128), "mn": _sb(NB), "dd": _sb(NB), "base": _sb(NB, "float32"),
     "hb": _sb(3 * NB), "lo": _sb(3 * NB), "b3": _sb(3 * NB, "float32"),
     "RL": ("dram", [RO, 128, HB], "uint16"),
-    "RX0": ("dram", [16, 128, HB], "uint16"), "RX1": ("dram", [16, 128, HB], "uint16"), "RX2": ("dram", [16, 128, HB], "uint16"),
 }
+for _k in range(2 * RO):
+    SCRATCH["RX%d" % _k] = ("dram", [8, 128, HB], "uint16")
 PSUM = ("pe0", "pe1", "pe2", "pe3", "pg", "pa", "pb", "pc")
 for _k in PSUM:
     SCRATCH[_k] = ("psum", [128, 512], "float32")
 NDMA = 48
-SEMAPHORES = ["qv", "qs", "qp", "qg", "sent"] + ["rx%d" % t for t in range(RO)] + ["d%d" % k for k in range(NDMA)]
+SEMAPHORES = ["qv", "qs", "qp", "qg", "sent"] + ["rx%d" % t for t in range(2 * RO)] + ["d%d" % k for k in range(NDMA)]
 
 
 def _bits(engines):
@@ -73,12 +76,13 @@ def helper_program(g, core, src, half, dests, T, topo):
     rank = T.rank_of(src)
     eng = [e for e in topo.engines(core, dests[0]) if all(e in topo.engines(core, d) for d in dests)]
     for t in range(RO):
-        g.wait_ge(T.sem["rx%d" % t], 4)
+        u = 2 * t + half
+        g.wait_ge(T.sem["rx%d" % u], 8)
         tr = []
         for k, d in enumerate(dests):
             rid, pid = topo.addr(d, core)
             tr.append(RemoteDMATransfer(dst_ids=[DstId(rid=rid, pnc=pid)], dma_engine_mask=_bits(eng[2 * k:2 * k + 2]),
-                                        remote_sem=T.sem["rx%d" % t], src=T.RL[t], dst=T["RX%d" % t][2 * rank + half]))
+                                        remote_sem=T.sem["rx%d" % u], src=T.RL[t], dst=T["RX%d" % u][rank]))
         g.remote_dma_fused(tr, local_sem=T.sem.sent)
     g.wait_ge(T.sem.sent, RO * 2 * len(dests))
 
@@ -238,12 +242,11 @@ def rank_program(g, core, T, topo):
     H2 = NN // 2
     CH = 384
 
-    dma("s", R("qi"), (T.q[:, :], None))
-    for k in range(4):
-        dma("y", R("X0", XP + 2 * CH * k, XP + 2 * CH * (k + 1)), (T.z[:, 2 * CH * k:2 * CH * (k + 1)], None))
     dma("s", R("X0", XP - 2, XP), (T.z[:, V - 2:V], None))
-    dma("s", R("wb", 0, 1), (T.wt[:], None))
-    dma("s", R("X0", XP + V, XP + V + 2), (T.z[:, 0:2], None))
+    dma("s", R("qi"), (T.q[:, :], None))
+    for k in range(2):
+        dma("y", R("X0", XP + NN * k, XP + NN * (k + 1)), (T.z[:, NN * k:NN * (k + 1)], None))
+    dma("y", R("wb", 0, 1), (T.wt[:], None))
 
     iota(R("CI", 0, 1), [[1, 1]], 0, 1, fl=False)
     iota(R("J"), [[1, 144]], 0, 0)
@@ -252,6 +255,7 @@ def rank_program(g, core, T, topo):
     iota(R("J8"), [[0, 16], [16, 8]], 0, 0)
     iota(R("JM"), [[16, 8], [0, 4], [1, 4]], 0, 0)
     iota(R("JC"), [[16, 8], [0, 2], [1, 8]], 0, 0)
+    fill(R("K0"), NN)
     fill(S("WS", 1, NN, 2), NN)
 
     nbank = [0]
@@ -262,15 +266,25 @@ def rank_program(g, core, T, topo):
         mms([(R(ps, 0, n), R("IDN"), S(x, pos, n, 2)), (R(ps, 0, n), R("IDM"), S(x, neg, n, 2))])
         act(S(out, a, n, step), R(ps, 0, n), fn=F.Relu)
 
-    def relus(x, par, j):
+    def edge(x, par, j):
         c = XP + par + 2 * CH * j
         relu("EB%d" % par, c - XP + 15, CH + (1 if j == 3 and par == 0 else 0), x, c, c - 1, 2)
+
+    def right(x, par, j):
+        c = XP + par + 2 * CH * j
         relu("R2", CH * j, CH, x, c + 1, c)
+
+    def span(x, par, j):
+        c = XP + par + 2 * CH * j
         relu("R3", CH * j, CH, x, c + 1, c - 1)
 
+    GB = ("pg", "pb")
+
     def term(buf, z, a, b, first=False, last=False, at=0, step=1):
-        mms(([(R("pg", 0, NB), R("IDN"), R("OF"))] if first else [])
-            + [(R("pg", 8 * c, 8 * c + 8), S(buf, at + step * 128 * c, 128, step), R(z)) for c in range(a // 128, b // 128)], first, last)
+        ps = GB[a // H2]
+        mms(([(R(ps, 0, HB), R("IDN"), R("OF", 0, HB))] if first else [])
+            + [(R(ps, 8 * (c % 6), 8 * (c % 6) + 8), S(buf, at + step * 128 * c, 128, step), R(z)) for c in range(a // 128, b // 128)],
+            first, last)
 
     def terms(par, j, first=False):
         term("EB%d" % par, "ZWP", CH * j, CH * j + CH, first=first, at=15 + par, step=2)
@@ -296,94 +310,145 @@ def rank_program(g, core, T, topo):
     def lists():
         cp(R("LA"), R("pa", 0, NB))
         ts(R("LA1"), R("pa", 0, NB), 1.0, A.add)
-        cp(R("KI"), R("pa", 0, NB))
 
-    def gathered(x, par):
+    def gathered(t, x, rest):
+        par = t % 2
         ta(x, par, 0, H2)
+        if t == 0:
+            ts(R("ZWP"), R("J", 0, 128, 16), col(cG), A.is_equal, col(cW), A.mult)
+            ts(R("ZWN"), R("ZWP"), -1.0, A.mult)
         tb(x, par, 0, H2)
-        ta(x, par, H2, NN)
         te("s", par, 0, H2)
-        te("s", par, H2, NN)
+        if t == 0:
+            for fn, j in rest:
+                fn(x, par, j)
+        terms(par, 0, first=True)
+        terms(par, 1)
+        if t:
+            for fn, j in rest:
+                fn(x, par, j)
         term("TA", "ZWP", 0, H2)
         term("TB", "ZWN", 0, H2)
-        term("TA", "ZWP", H2, NN)
-        term("TE", "ZWP", 0, H2)
+        term("TE", "ZWP", 0, H2, last=True)
+        if t:
+            ta(x, par, H2, NN)
+        else:
+            ms(R("WN3", 0, NN), 0.0)
+        send(2 * t)
+        if t == 0:
+            ta(x, par, H2, NN)
+        te("s", par, H2, NN - 256)
+        te("s", par, NN - 256, NN)
         tb(x, par, H2, NN - 256)
-        term("TB", "ZWN", H2, NN - 256)
-        term("TE", "ZWP", H2, NN)
         tb(x, par, NN - 256, NN)
-        term("TB", "ZWN", NN - 256, NN, last=True)
+        terms(par, 2, first=True)
+        terms(par, 3)
+        term("TA", "ZWP", H2, NN)
+        term("TB", "ZWN", H2, NN - 256)
+        term("TE", "ZWP", H2, NN - 256)
+        term("TB", "ZWN", NN - 256, NN)
+        term("TE", "ZWP", NN - 256, NN, last=True)
+        send(2 * t + 1)
 
     hs = helpers(core, T, topo)
 
-    def send(t):
-        s = R("SND", t * NB, (t + 1) * NB)
-        cp(s, R("pg", 0, NB))
-        deps("g", [s[1]], [], ("sent", 16 * (t + 1)))
+    def send(u):
+        s = R("SND", u * HB, (u + 1) * HB)
+        cp(s, R(GB[u % 2], 0, HB))
+        deps("g", [s[1]], [], ("sent", 16 * (u + 1)))
         tr = []
-        for k, (c, half, dests) in enumerate(hs):
+        for k, c in enumerate([c for c, half, dests in hs if half == u % 2]):
             rid, pid = topo.addr(c, core)
-            tr.append(RemoteDMATransfer(dst_ids=[DstId(rid=rid, pnc=pid)], dma_engine_mask=_bits(topo.engines(core, c)[4 * k:4 * k + 4]),
-                                        remote_sem=T.sem["rx%d" % t], src=T.SND[:, t * NB + half * HB:t * NB + (half + 1) * HB], dst=T.RL[t]))
+            tr.append(RemoteDMATransfer(dst_ids=[DstId(rid=rid, pnc=pid)], dma_engine_mask=_bits(topo.engines(core, c)[8 * k:8 * k + 8]),
+                                        remote_sem=T.sem["rx%d" % u], src=s[0], dst=T.RL[u // 2]))
         g.remote_dma_fused(tr, local_sem=T.sem.sent)
 
-    def guests(par):
-        cp(X(R("WS"), R("LA")), R("K1"))
+    def guests(par, n):
+        act(X(R("WS", 0, V), R("LA", 0, n)), R("K0", 0, 16 * n), fn=F.Silu)
+        act(R("ST"), S("WS", 1 - par, NN, 2))
+        if n < NB:
+            cp(X(R("WB"), R("LA", n, NB)), R("K1", 16 * n, NN))
 
-    def moves(par):
-        ts(R("P1"), R("KI"), 1, A.logical_shift_right, 15, A.bitwise_and)
-        ts(R("P2"), R("KI"), 5, A.logical_shift_right)
-        ts(R("PA"), R("P1"), 288.0, A.mult, float(NB), A.add)
-        tt(R("PB"), R("P2"), R("SB%d" % par), A.subtract)
-        tt(R("DS"), R("PA"), R("PB"), A.add)
+    def moves(par, part):
+        if part == 0:
+            cp(R("KI"), R("LA"))
+            ts(R("P1"), R("KI"), 1, A.logical_shift_right, 15, A.bitwise_and)
+            ts(R("P2"), R("KI"), 5, A.logical_shift_right)
+        else:
+            ts(R("PA"), R("P1"), 288.0, A.mult, float(NB), A.add)
+            tt(R("PB"), R("P2"), R("SB%d" % par), A.subtract)
+            tt(R("DS"), R("PA"), R("PB"), A.add)
 
     def records(t):
-        par = t % 2
         for j in range(4):
-            ps = "pe%d" % j
-            lst = [(R(ps, 0, CH), R("RS"), R("K1", CH * j, CH * j + CH))]
+            ps, a = "pe%d" % j, CH * j
+            lst = [(R(ps, 0, CH), R("RS"), R("K1", a, a + CH))]
             if t == 0:
-                src = "TA" if j < 2 else "TB"
-                lst += [(S(ps, r // 2, HB, 8), R("RQ" if r % 2 else "RC"), R(src, NB * r + HB * (j % 2), NB * r + HB * (j % 2) + HB))
-                        for r in range(16)]
+                lst += [(S(ps, r // 2, HB, 8), R("RQ0" if r % 2 else "RC0", rows=16),
+                         R("KQ", 192 * r + HB * j, 192 * r + HB * j + HB, rows=16)) for r in range(16)]
             else:
-                lst += [(R(ps, 0, CH), R("RC"), R("QC", CH * j, CH * j + CH)),
-                        (R(ps, 0, CH), R("RQ"), R("QO", CH * j + par, CH * j + CH + par))]
+                lst += [(R(ps, 0, CH), R("RC"), R("QC", a, a + CH))]
             mms(lst, last=False)
-        if par:
-            mms([(R("pc", 0, 1), R("RQ"), R("QO", 0, 1))])
-            act(R("T2", 15, 16), R("pc", 0, 1))
+
+    def targets(t, h):
+        par = t % 2
+        for j in (2 * h, 2 * h + 1):
+            mms([(R("pe%d" % j, 0, CH), R("RQ"), R("QO", CH * j + par, CH * j + CH + par))], False, False)
+        if par and h == 0:
+            mms([(R("pa", 0, 1), R("RQ"), R("QO", 0, 1))])
+            cp(R("T2", 15, 16), R("pa", 0, 1))
+
+    def keep(q, buf, j, bias):
+        rl(q, R(buf, 16 + CH * j, 16 + CH * j + CH), R("pe%d" % j, 0, CH), col(bias))
+
+    def fetch(u):
+        wait("y", "rx%d" % u, 2 * len(T.cores))
+        dma("y", R("RXS", CH * (u % 2), CH * (u % 2) + CH), (T["RX%d" % u][:], None))
+
+    def arrive(t, h):
+        par, ps, a = t % 2, ("pg", "pc")[h], CH * h
+        for k0, k1 in ((0, 1), (1, 4)):
+            cp(R("RXF", a + NB * k0, a + NB * k1), R("RXS", a + NB * k0, a + NB * k1))
+            mms([(S(ps, k, 16, 4, NB), R("RXF", a + NB * k, a + NB * k + NB), R("RM")) for k in range(k0, k1)], k0 == 0, k1 == 4)
+        if h:
+            if t:
+                targets(t, 1)
+            keep("v", "Y", 0, cY0 + par)
+            cp(R("LI"), R("pb", 0, NB))
+        else:
+            moves(par, 0)
+        mc = R("mc", 64 * h, 64 * h + 64, rows=NB)
+        ts(mc, R(ps, 0, 64, rows=NB), float(8 * OFF), A.is_gt)
+        for j in range(2):
+            mms([(S("pe%d" % (2 * h + j), 128 * (c % 3) + e, 64, 2), R("E12", 128 * (6 * e + c), 128 * (6 * e + c) + 128, rows=NB), mc)
+                 for c in range(3 * j, 3 * j + 3) for e in range(2)], first=False)
+        keep("s", "Y", 1 + h, cY0 + par)
+        if h:
+            moves(par, 1)
+            keep("v", "Y", 3, cY0 + par)
 
     def decide(t):
         par = t % 2
-        wait("y", "rx%d" % t, 4 * len(T.cores))
-        dma("y", R("RXS"), (T["RX%d" % t][:], None))
-        cp(R("LI"), R("pb", 0, NB))
-        for a, b in ((0, 2), (2, 5), (5, 8)):
-            cp(R("RXF", NB * a, NB * b), R("RXS", NB * a, NB * b))
-            mms([(R("pg", k, 128, 8, NB), R("RXF", NB * k, NB * k + NB), R("RM")) for k in range(a, b)], a == 0, b == 8)
-        ts(R("mc", rows=NB), R("pg", 0, 128, rows=NB), float(8 * OFF), A.is_gt)
-        for j in (0, 2, 1, 3):
-            lst = []
-            for c in range(3 * j, 3 * j + 3):
-                for e in (0, 1):
-                    x = 6 * e + c % 6
-                    lst.append((R("pe%d" % j, 128 * (c % 3) + e, 128 * (c % 3) + 128, 2), R("E12", 128 * x, 128 * x + 128, rows=NB),
-                                R("mc", 64 * (c // 6), 64 * (c // 6) + 64, rows=NB)))
-            mms(lst, first=False)
-        for j in range(4):
-            rl("s" if j < 2 else "v", R("Y", 16 + CH * j, 16 + CH * j + CH), R("pe%d" % j, 0, CH), col(cY0 + par))
+        fetch(2 * t)
+        fetch(2 * t + 1)
+        if t:
+            mms([(R("pb", 0, NB), zl("ZQ", r), S("WB", 1 - par + 2 * r, NB, 32)) for r in range(16)], last=False)
+            targets(t, 0)
+            arrive(t, 0)
+        mms([(R("pb", 0, NB), zl("ZQ", r), S("ST", r, NB, 16)) for r in range(16)], first=(t == 0))
+        if t == 0:
+            arrive(t, 0)
+        arrive(t, 1)
         tile("pa", "ZG", "Y", 16)
-        GS = 48
-        act(R("T3", 0, 16 * GS), X(R("Y"), R("LI", 0, GS)))
-        cp(R("T3", 16 * GS, NN), X(R("Y"), R("LI", GS, NB)))
-        tile("pb", "ZG", "T3")
+        for k in range(4):
+            mv("sv"[k % 2], R("T3", CH * k, CH * k + CH), X(R("Y"), R("LI", QB * k, QB * k + QB)))
+        for h in range(2):
+            mms([(R("pb", HB * h, HB * h + HB), zl("ZG", r), S("T3", H2 * h + r, HB, 16)) for r in range(16)], h == 0, h == 1)
         cp(R("mn"), R("pa", 0, NB))
-        for j in range(3):
-            rl("s", R("T2", 16 + CH * j, 16 + CH * j + CH), R("pe%d" % j, 0, CH), col(cT0 + par))
-        rl("v", R("T2", 16 + CH * 3, 16 + NN), R("pe3", 0, CH), col(cT0 + par))
+        for j in range(4):
+            keep("s" if j else "v", "T2", j, cT0 + par)
         if par:
-            rl("v", R("W", 16 + V, 17 + V), R("pe3", CH - 1, CH), col(cT0 + par))
+            rl("s", R("W", 16 + V, 17 + V), R("pe3", CH - 1, CH), col(cT0 + par))
         tt(R("S2"), R("mn"), R("DS"), A.mult)
         tt(R("dd"), R("pb", 0, NB), R("mn"), A.subtract)
         mms([(R("pc", 0, NB), R("TLT"), R("dd")), (R("pc", 1, NB), R("TGE"), R("dd", 0, NB - 1))]
@@ -402,14 +467,18 @@ def rank_program(g, core, T, topo):
             for k, d in enumerate((0.0, 1.0, -1.0)):
                 act(R("lo", k * NB, k * NB + NB), R("pa", 0, NB), bias=d)
             dma("s", row("WN3", 1, 0, 3 * NN), R("lo"))
+            if t == 0:
+                odd_round()
             w3, w2 = "WN3", "WN2"
         else:
             for k, d in enumerate((0.0, 1.0, -1.0)):
                 act(R("b3", k * NB, k * NB + NB), R("base"), bias=d)
-            dma("s", row("WF3", 0, 0, 3 * NN), R("b3"))
-            w3, w2 = "WF3", "WF2"
+            dma("s", row("WS", 0, 0, 3 * NN), R("b3"))
+            w3, w2 = "WS", "WF2"
         act(S(w2, par, NN, 2), X(R(w3), R("LS")))
-        act(S(w2, 1 - par, NN, 2), X(R(w3), R("LSO")))
+        OS = 64
+        act(S(w2, 1 - par, 16 * OS, 2), X(R(w3), R("LSO", 0, OS)))
+        cp(S(w2, 1 - par + 32 * OS, NN - 16 * OS, 2), X(R(w3), R("LSO", OS, NB)))
 
         def w(s):
             return S("W", 16 + s, NB, 32)
@@ -430,37 +499,35 @@ def rank_program(g, core, T, topo):
     ts(R("CI", 1, 2), R("CI", 0, 1), 15, A.bitwise_and)
     cp(col(cP), R("CI", 0, 1))
     cp(col(cR), R("CI", 1, 2))
-    ms(S("EB0", 16, NN, 2), -200.0)
+    for k in range(12):
+        act(S("EB0", 16 + 256 * k, 128, 2), R("J", 0, 128), scale=0.0, bias=-200.0)
     tt(col(cG), col(cP), col(cR), A.subtract)
+    ts(col(cK), col(cR), float(NB), A.mult)
     ts(R("IDN"), R("J", 0, 128), col(cP), A.is_equal)
     ts(col(cTQ), col(cG), 4.0, A.mult, col(cR), A.add)
     ts(R("IDM"), R("J", 0, 128), col(cP), A.is_equal, -1.0, A.mult)
+    ts(R("KI"), R("J", 0, NB), col(cK), A.add)
     for k in range(2):
         ts(R("SEL", 128 * k, 128 * k + 128), R("JJ"), col(cTQ), A.subtract, float(16 * k), A.is_equal)
+    ts(R("P2"), R("KI"), 63, A.bitwise_and)
+    ts(R("P1"), R("KI"), 4032, A.bitwise_and)
     ts(col(cT15), col(cG), 15.0, A.add)
-    ts(col(cK), col(cR), float(NB), A.mult)
-    ms(R("OF"), float(OFF))
-    cp(R("qf"), R("qi"))
-    mms([(R("pa", 0, NB), R("SEL", 128 * k, 128 * k + 128), S("qf", k, NB, 2)) for k in range(2)])
-    ts(R("P1"), R("J", 0, NB), col(cK), A.add)
-    ms(R("K1"), 0.0)
-    ts(R("P2"), R("P1"), 63, A.bitwise_and)
-    ts(R("P1"), R("P1"), 4032, A.bitwise_and)
     ts(R("KB", NB, 2 * NB), R("P2"), 16.0, A.add)
     cp(R("KB", 0, NB), R("P1"))
-    lists()
-    for k in range(2):
-        dma("y", row("K1", k), R("KB", k * NB, k * NB + NB))
-    cp(col(cW), R("wb", 0, 1))
+    ms(col(cH), -12.0)
+    cp(R("qf"), R("qi"))
+    mms([(R("pa", 0, NB), R("SEL", 128 * k, 128 * k + 128), S("qf", k, NB, 2)) for k in range(2)])
+    act(R("qh", 0, 192), R("qf"), bias=col(cH), fn=F.Relu)
+    ms(R("OF"), float(OFF))
     ts(R("LT", 0, 17), R("J", 0, 17), col(cR), A.is_gt)
-    ts(R("ZWP"), R("J", 0, 128, 16), col(cG), A.is_equal, col(cW), A.mult)
     ts(R("RM"), R("J", 0, 16), col(cR), A.is_equal)
-    ts(R("ZWN"), R("ZWP"), -1.0, A.mult)
     ts(R("ZQ"), R("J"), col(cT15), A.is_equal, lt(2), A.mult)
-    ts(R("qa"), R("qi"), 4032, A.bitwise_and)
-    ts(R("qb"), R("qi"), 63, A.bitwise_and)
-    cp(R("qh", 0, 192), R("qa"))
-    cp(R("qh", 192, 384), R("qb"))
+    lists()
+    tt(R("qh", 192, 384), R("qf"), R("qh", 0, 192), A.subtract)
+    for k in range(2):
+        dma("y", row("K0", k), R("KB", k * NB, k * NB + NB))
+    for f in range(2):
+        dma("y", (T.KQ[8 * f:8 * f + 8, :], ("KQ", 0, V, ("row", f))), R("qh", 192 * f, 192 * f + 192))
 
     def matrices():
         ts(R("B8"), R("J8"), col(cG), A.is_equal)
@@ -470,9 +537,6 @@ def rank_program(g, core, T, topo):
         cp(col(cX), R("CI", 3, 4))
         ts(R("DA"), R("J", 0, 128), col(cP), A.is_equal, col(cAL), A.mult)
         ts(R("RM8", 0, 12), R("J", 0, 96, 8), col(cX), A.is_equal)
-        mms([(R("pc", 0, 128), R("B8"), R("DA"))])
-        for r in range(12):
-            act(R("E12", 128 * r, 128 * r + 128), R("pc", 0, 128), scale=R("RM8", r, r + 1))
         ts(col(c2), lt(2), 2.0, A.mult)
         ts(col(cP2), col(cP), 2.0, A.add)
         ts(col(cP6), col(cP), 6.0, A.add)
@@ -498,45 +562,57 @@ def rank_program(g, core, T, topo):
         ts(col(cY), col(cY), col(cU), A.add)
         ts(col(cN), rm(5), col(cN), A.add)
         tt(col(cU), rm(1), rm(5), A.add)
-        for par in range(2):
-            ts(col(cY0 + par), rm(9), float(par - 32), A.mult, col(cY), A.add)
-            ts(col(cT0 + par), col(cU), float(par - 32), A.mult, col(cN), A.add)
-            ts(col(cI0 + par), col(cR), 2.0, A.mult, float(-31 - par), A.add)
+        ts(col(cSB), col(cR), 288.0, A.mult)
+        ts(col(cY0), rm(9), -32.0, A.mult, col(cY), A.add)
+        ts(col(cT0), col(cU), -32.0, A.mult, col(cN), A.add)
+        ts(col(cI0), col(cR), 2.0, A.mult, -31.0, A.add)
+        ts(R("SB0"), R("J", 0, NB), col(cSB), A.add, 192.0, A.add)
+        ts(R("LSO"), R("J", 0, NB), col(cSB), A.add)
         ms(R("C32"), 32.0)
         ms(R("ZR"), 0.0)
-        ms(col(cH), -12.0)
         ms(R("Y", 0, 16), 0.0)
-        ms(R("QO", NN, NN + 16), 0.0)
-        ts(col(cSB), col(cR), 288.0, A.mult)
-        ts(R("LSO"), R("J", 0, NB), col(cSB), A.add)
-        ts(R("SB0"), R("J", 0, NB), col(cSB), A.add, 192.0, A.add)
-        ts(col(cY), rm(15), float(1 - 288 * 16), A.mult, col(cSB), A.add)
-        ts(R("SB1"), R("J", 0, NB), col(cY), A.add, 480.0, A.add)
-        ts(R("SB1", NB - 1, NB), rm(15), float(3 * NN - 288), A.mult, R("SB1", NB - 1, NB), A.add)
-        ts(col(cY), rm(0), 3008.0, A.mult)
-        ts(col(cU), rm(1), 63.0, A.mult, col(cY), A.add)
-        ts(R("WN3", 3 * NN, 3 * NN + 16), R("C32", 0, 16), 0.0, A.mult, col(cU), A.add)
 
+    def odd_round():
+        act(col(cX), rm(0), scale=3008.0)
+        act(col(cY), rm(15), scale=float(1 - 288 * 16), bias=col(cSB))
+        act(col(cY1), rm(9), bias=col(cY0))
+        act(col(cN), rm(1), scale=63.0, bias=col(cX))
+        act(col(cK), col(cY), bias=480.0)
+        act(col(cT1), col(cU), bias=col(cT0))
+        act(R("WN3", 3 * NN, 3 * NN + 16), R("C32", 0, 16), scale=0.0, bias=col(cN))
+        act(R("SB1"), R("J", 0, NB), bias=col(cK))
+        act(col(cI1), col(cI0), bias=-1.0)
+        act(col(cX), rm(15), scale=float(3 * NN - 288), bias=R("SB1", NB - 1, NB))
+        act(R("QO", NN, NN + 16), R("C32", 0, 16), scale=0.0)
+        act(R("SB1", NB - 1, NB), col(cX))
+
+    matrices()
     for j in range(4):
         own("v", "X0", 0, j)
-        relus("X0", 0, j)
-        if j:
-            terms(0, j - 1, first=(j == 1))
-    terms(0, 3)
-    gathered("X0", 0)
-    send(0)
+        if j == 0:
+            cp(R("X0", XP + V, XP + V + 1), R("X0", XP, XP + 1))
+        edge("X0", 0, j)
+        if j < 2:
+            right("X0", 0, j)
+            span("X0", 0, j)
+    cp(col(cW), R("wb", 0, 1))
+    gathered(0, "X0", [(right, 2), (span, 2), (right, 3), (span, 3)])
     fill(R("W"), XW)
-    fill(R("WN3", 0, 3 * NN), 3 * NN)
+    fill(R("WN3", NN, 3 * NN), V)
     fill(S("EB1", 17, NN, 2), NN, -200)
-    for k, (buf, a) in enumerate((("TA", 0), ("TB", NB))):
-        for f in range(2):
-            dma("y", row(buf, f), R("qh", 192 * f + a, 192 * f + a + NB))
-    matrices()
-    guests(0)
+    guests(0, NB)
+    cp(R("K1"), R("K0"))
+    ts(R("CI", 5, 6), R("CI", 0, 1), 7, A.bitwise_and)
+    ts(R("CI", 6, 7), R("CI", 0, 1), 3, A.logical_shift_right)
+    ts(col(cU), R("CI", 5, 6), 16.0, A.mult, 2.0, A.add)
+    ts(col(cX), R("CI", 6, 7), col(cU), A.add)
+    ts(R("RC0"), R("JC"), col(cX), A.is_equal)
+    ts(R("RQ0"), R("J", 0, 128), col(cX), A.subtract, 4.0, A.is_equal)
+    mms([(R("pc", 0, 128), R("B8"), R("DA"))])
+    for r in range(12):
+        ts(R("E12", 128 * r, 128 * r + 128), R("pc", 0, 128), R("RM8", r, r + 1), A.mult)
     records(0)
-    tile("pb", "ZQ", "WS", 1, 2)
     matrices2()
-    moves(0)
 
     for t in range(RO):
         xo, xn = "X%d" % (t % 2), "X%d" % ((t + 1) % 2)
@@ -545,54 +621,66 @@ def rank_program(g, core, T, topo):
         decide(t)
         if t < RO - 1:
             fill(S("WS", 1 - par, NN, 2), NN)
+            fill(S("WB", 1 - par, NN, 2), NN)
             turn("pa", 0, par, 1)
-            turn("pb", 0, 0, 0)
-            turn("pb", NB, 1, 0)
-            turn("pc", 0, 1 - par, 1)
+            turn("pb", 0, 1 - par, 0)
+            turn("pc", 0, par, 0)
+            turn("pg", 0, 1 - par, 1)
             cp(R("LQ", 0, NB), R("pa", 0, NB))
-            cp(R("LX"), R("pb", 0, 2 * NB))
+            cp(R("LX", 0, NB), R("pb", 0, NB))
             act(R("QC"), X(R("WN2"), R("LQ", 0, NB)))
+
+            def others(a, b):
+                cp(S(xn, XP + 1 - par + 32 * a, 16 * (b - a), 2), X(win, R("LX", a, b)))
+
+            def cands(a, b):
+                cp(S(xn, XP + par + 32 * a, 16 * (b - a), 2), X(win, R("LX", NB + a, NB + b)))
+                for j in range(a // QB, b // QB):
+                    own("g", xn, par, j)
+
+            def wrap():
+                cp(R(xn, XP + V, XP + V + 1), R(xn, XP, XP + 1))
+
             if par == 0:
-                cp(R(xn, 0, XP), X(win, R("LX", 2 * NB - 2, 2 * NB)))
-
-            def xs(j):
-                for e in range(2):
-                    cp(S(xn, XP + e + 2 * CH * j, CH, 2), X(win, R("LX", NB * e + 24 * j, NB * e + 24 * j + 24)))
-                own("g", xn, par, j)
-                if j == 0:
-                    cp(R(xn, XP + V, XP + V + 1), R(xn, XP, XP + 1))
-
-            xs(0)
-            cp(R("LQ", NB, 2 * NB), R("pc", 0, NB))
-            xs(1)
-            relus(xn, par, 0)
+                cp(R(xn, 0, XP), X(win, R("LX", NB - 2, NB)))
+            others(0, HB + 2 * par)
+            cp(R("LX", NB, 2 * NB), R("pc", 0, NB))
+            cp(R("LQ", NB, 2 * NB), R("pg", 0, NB))
+            span(xn, par, 0)
+            span(xn, par, 1)
+            cands(0, QB)
+            wrap()
+            edge(xn, par, 0)
+            right(xn, par, 0)
+            cands(QB, HB)
             tile("pa", "ZQ", "QC")
-            xs(2)
-            relus(xn, par, 1)
+            edge(xn, par, 1)
+            right(xn, par, 1)
+            others(HB + 2 * par, NB)
+            span(xn, par, 2)
+            span(xn, par, 3)
+            cands(HB, NB)
             lists()
-            xs(3)
-            relus(xn, par, 2)
-            relus(xn, par, 3)
-            for j in range(4):
-                terms(par, j, first=(j == 0))
-            gathered(xn, par)
-            send(t + 1)
+            edge(xn, par, 2)
+            edge(xn, par, 3)
+            gathered(t + 1, xn, [(right, 2), (right, 3)])
             fill(R("W"), XW)
             if t == 0:
-                fill(R("WF3"), 3 * NN)
-            act(R("QO", 0, NN), X(R("WN2"), R("LQ", NB, 2 * NB)))
-            guests(par)
+                fill(R("WS", V, 3 * NN), NN)
+            guests(par, 60)
+            for q, a, b in (("v", 0, HB + 2), ("s", HB + 2, NB)):
+                mv(q, R("QO", 16 * a, 16 * b), X(R("WN2"), R("LQ", NB + a, NB + b)))
             records(t + 1)
-            tile("pb", "ZQ", "WS", 1 - par, 2)
-            moves(par)
         else:
-            turn("pa", 0, 0, 0)
-            turn("pa", NB, 1, 0)
-            turn("pb", 0, 0, 1)
-            turn("pb", NB, 1, 1)
-            cp(R("LX"), R("pa", 0, 2 * NB))
-            cp(R("LQ"), R("pb", 0, 2 * NB))
+            turn("pa", 0, 1, 0)
+            turn("pb", 0, 0, 0)
+            turn("pc", 0, 0, 1)
+            turn("pc", NB, 1, 1)
+            cp(R("LX", NB, 2 * NB), R("pa", 0, NB))
+            cp(R("LX", 0, NB), R("pb", 0, NB))
             for j in range(4):
+                if j == 1:
+                    cp(R("LQ"), R("pc", 0, 2 * NB))
                 for e, q in enumerate("vs"):
                     mv(q, S(xn, XP + e + 2 * CH * j, CH, 2), X(win, R("LX", NB * e + 24 * j, NB * e + 24 * j + 24)))
                 dma("y", (T.yz[:, 2 * CH * j:2 * CH * (j + 1)], None), R(xn, XP + 2 * CH * j, XP + 2 * CH * (j + 1)))
@@ -605,4 +693,4 @@ def rank_program(g, core, T, topo):
         wait("y", "d%d" % k, 16)
     for q in cnt:
         wait("y", "q" + q, cnt[q])
-    g.wait_ge(T.sem.sent, 16 * RO)
+    g.wait_ge(T.sem.sent, 32 * RO)

from concourse.bass import DstId, RemoteDMATransfer
from concourse.mybir import AluOpType, ActivationFunctionType

A = AluOpType
F = ActivationFunctionType
NN = 1536
V = 2 * NN
NB = 96
HB = 48
QB = 24
XW = V + 32
XP = 32
OFF = 22400
BIG = 4096.0
RO = 3


def _sb(w, d="bfloat16"):
    return ("sbuf", [128, w], d)


SCRATCH = {
    "X0": _sb(XP + V + 16), "X1": _sb(XP + V + 16), "EB0": _sb(XW), "EB1": _sb(XW), "W": _sb(XW),
    "WS": _sb(3 * NN, "float32"), "WB": _sb(V), "K0": _sb(NN, "float32"), "ST": _sb(NN),
    "ZR": _sb(NB), "XC": _sb(NN), "R2": _sb(NN), "R3": _sb(NN), "TA": _sb(NN), "TB": _sb(NN), "TE": _sb(NN),
    "Y": _sb(NN + 16), "T2": _sb(NN + 16), "T3": _sb(NN), "K1": _sb(NN), "QC": _sb(NN), "QO": _sb(NN + 16),
    "WN3": _sb(3 * NN + 16), "WN2": _sb(V), "WF2": _sb(V, "float32"), "QF": _sb(V, "float32"),
    "RXS": _sb(768, "uint16"), "RXF": _sb(768, "float32"), "E12": _sb(1536), "OF": _sb(NB),
    "SND": _sb(RO * NB, "uint16"), "TW": _sb(512, "float32"),
    "qi": _sb(192, "int32"), "qf": _sb(192, "float32"), "qa": _sb(192, "int32"), "qb": _sb(192, "int32"), "qh": _sb(384),
    "wb": _sb(8), "C": _sb(64, "float32"), "CI": _sb(8, "int32"), "LT": _sb(24, "float32"), "RM": _sb(16, "float32"),
    "RM8": _sb(16, "float32"), "J": _sb(144, "float32"), "J16": _sb(128, "float32"), "J8": _sb(128, "float32"),
    "JJ": _sb(128, "float32"), "JM": _sb(128, "float32"), "JC": _sb(128, "float32"), "SEL": _sb(256, "float32"),
    "ZWP": _sb(8), "ZWN": _sb(8), "ZQ": _sb(144), "ZG": _sb(144), "IDF": _sb(128, "float32"), "SELW": _sb(48),
    "BLK": _sb(128), "B8": _sb(128), "TLT": _sb(128), "TGE": _sb(128), "IDN": _sb(128), "IDM": _sb(128), "DA": _sb(128),
    "RS": _sb(128), "RC": _sb(128), "RQ": _sb(128), "RC0": _sb(128), "RQ0": _sb(128), "KQ": _sb(V), "KB": _sb(2 * NB, "float32"),
    "KI": _sb(NB, "int32"), "P1": _sb(NB, "int32"), "P2": _sb(NB, "int32"), "PA": _sb(NB, "float32"), "PB": _sb(NB, "float32"),
    "LA": _sb(NB, "uint16"), "LA1": _sb(NB, "uint16"), "LI": _sb(NB, "uint16"), "LS": _sb(NB, "uint16"),
    "LB": _sb(NB, "uint16"), "LSO": _sb(NB, "uint16"), "LX": _sb(2 * NB, "uint16"), "LQ": _sb(2 * NB, "uint16"),
    "SB0": _sb(NB, "float32"), "SB1": _sb(NB, "float32"), "DS": _sb(NB, "float32"), "S2": _sb(NB, "float32"),
    "C32": _sb(NB, "float32"), "mc": _sb(128), "mn": _sb(NB), "dd": _sb(NB), "base": _sb(NB, "float32"),
    "hb": _sb(3 * NB), "lo": _sb(3 * NB), "b3": _sb(3 * NB, "float32"),
    "RL": ("dram", [RO, 128, HB], "uint16"),
}
for _k in range(2 * RO):
    SCRATCH["RX%d" % _k] = ("dram", [8, 128, HB], "uint16")
PSUM = ("pe0", "pe1", "pe2", "pe3", "pg", "pa", "pb", "pc")
for _k in PSUM:
    SCRATCH[_k] = ("psum", [128, 512], "float32")
NDMA = 48
SEMAPHORES = ["qv", "qs", "qp", "qg", "sent"] + ["rx%d" % t for t in range(2 * RO)] + ["d%d" % k for k in range(NDMA)]


def _bits(engines):
    m = 0
    for e in engines:
        m |= 1 << e
    return m


def helpers(rank_core, T, topo):
    far = [d for d in T.cores if d != rank_core and not topo.may_write(rank_core, d)]
    near = [d for d in T.cores if d not in far]
    free = [c for c in topo.cores_of(rank_core) if c not in T.cores]
    out = []
    for half, die in enumerate(sorted(set(topo.die(c) for c in free))):
        mine = [c for c in free if topo.die(c) == die]
        port = [c for c in mine if all(topo.may_write(c, d) for d in far)][0]
        rest = [c for c in mine if c != port and all(topo.may_write(c, d) for d in near)][0]
        out.append((port, half, far))
        out.append((rest, half, near))
    return out


def helper_program(g, core, src, half, dests, T, topo):
    rank = T.rank_of(src)
    eng = [e for e in topo.engines(core, dests[0]) if all(e in topo.engines(core, d) for d in dests)]
    for t in range(RO):
        u = 2 * t + half
        g.wait_ge(T.sem["rx%d" % u], 8)
        tr = []
        for k, d in enumerate(dests):
            rid, pid = topo.addr(d, core)
            tr.append(RemoteDMATransfer(dst_ids=[DstId(rid=rid, pnc=pid)], dma_engine_mask=_bits(eng[2 * k:2 * k + 2]),
                                        remote_sem=T.sem["rx%d" % u], src=T.RL[t], dst=T["RX%d" % u][rank]))
        g.remote_dma_fused(tr, local_sem=T.sem.sent)
    g.wait_ge(T.sem.sent, RO * 2 * len(dests))


def rank_program(g, core, T, topo):
    rank = T.rank_of(core)
    if rank is None:
        for src in T.cores:
            if core in topo.cores_of(src):
                for c, half, dests in helpers(src, T, topo):
                    if c == core:
                        helper_program(g, core, src, half, dests, T, topo)
        return

    Q = {"v": g.vector, "s": g.scalar, "p": g.tensor, "g": g, "y": g.sync}
    cnt = {"v": 0, "s": 0, "p": 0, "g": 0}
    seen = {k: {} for k in Q}
    log = {}
    nd = [0]

    def wait(q, sem, val):
        if seen[q].get(sem, 0) < val:
            Q[q].wait_ge(T.sem[sem], val)
            seen[q][sem] = val

    def apart(x, y):
        return x is not None and y is not None and x[0] == y[0] and x[1] != y[1]

    def deps(q, rd, wr, tok):
        need = {}
        acc = [(r, False) for r in rd] + [(w, True) for w in wr]
        for (name, a, b, tag), w in acc:
            ps = name in PSUM
            for (a2, b2, tag2, w2, tok2) in log.get(name, []):
                if ps:
                    hit = tok2[0] != tok[0] or (q != "p" and (w or w2))
                else:
                    hit = a < b2 and a2 < b and (w or w2) and not apart(tag, tag2)
                    hit = hit and not (q == "p" and tok2[0] == "qp")
                if hit:
                    need[tok2[0]] = max(need.get(tok2[0], 0), tok2[1])
        for sem, val in need.items():
            wait(q, sem, val)
        for (name, a, b, tag), w in acc:
            old = log.get(name, [])
            if w and tag is None and name not in PSUM:
                old = [e for e in old if not (a <= e[0] and e[1] <= b)]
            log[name] = [e for e in old if not (e[4][0] == tok[0] and e[:4] == (a, b, tag, w))] + [(a, b, tag, w, tok)]

    def R(name, a=0, b=None, step=1, rows=128):
        t = T[name]
        if b is None:
            b = t.shape[1]
        tag = ("par", a % 2) if step % 2 == 0 else None
        return (t[0:rows, a:b:step] if step != 1 else t[0:rows, a:b], (name, a, b, tag))

    def S(name, a, n, step, rows=128):
        return R(name, a, a + step * (n - 1) + 1, step, rows)

    def row(name, r, a=0, b=NN):
        return (T[name][r::16, a:b], (name, a, b, ("row", r)))

    def X(win, off):
        return (win[0].indirect(off[0]), win[1], off[1])

    def run(q, fn, ins, outs, inc=True):
        rd, wr = [], []
        for x in ins:
            if isinstance(x, tuple):
                rd += list(x[1:])
        for x in outs:
            wr.append(x[1])
            rd += list(x[2:])
        tok = ("q" + q, cnt[q] + 1)
        deps(q, rd, wr, tok)
        call = fn()
        if inc:
            call.then_inc(T.sem["q" + q], 1)
            cnt[q] += 1

    def ap(x):
        return x[0] if isinstance(x, tuple) else x

    def cp(o, i):
        run("v", lambda: g.vector.tensor_copy(o[0], i[0]), [i], [o])

    def tt(o, a, b, op):
        run("v", lambda: g.vector.tensor_tensor(o[0], a[0], b[0], op), [a, b], [o])

    def ts(o, a, s1, op0, s2=None, op1=None):
        if op1 is None:
            run("v", lambda: g.vector.tensor_scalar(o[0], a[0], ap(s1), None, op0), [a, s1], [o])
        else:
            run("v", lambda: g.vector.tensor_scalar(o[0], a[0], ap(s1), ap(s2), op0, op1), [a, s1, s2], [o])

    def ms(o, val):
        run("v", lambda: g.vector.memset(o[0], val), [], [o])

    def scan(o, d0, d1, init, op0, op1):
        run("v", lambda: g.vector.tensor_tensor_scan(o[0], d0[0], d1[0], ap(init), op0, op1), [d0, d1, init], [o])

    def act(o, i, scale=None, bias=None, fn=None):
        kw = {}
        if scale is not None:
            kw["scale"] = ap(scale)
        if bias is not None:
            kw["bias"] = ap(bias)
        if fn is None:
            fn = F.Identity if isinstance(bias, tuple) else F.Copy
        run("s", lambda: g.scalar.activation(o[0], i[0], fn, **kw), [i, scale, bias], [o])

    def mv(q, o, i):
        (cp if q == "v" else act)(o, i)

    def rl(q, o, i, bias):
        if q == "v":
            ts(o, i, bias, A.add, 0.0, A.max)
        else:
            act(o, i, bias=bias, fn=F.Relu)

    def mms(lst, first=True, last=True):
        for k, (o, l, r) in enumerate(lst):
            st, en = first and k == 0, last and k == len(lst) - 1
            run("p", lambda: g.tensor.matmul(o[0], l[0], r[0], st, en), [l, r], [o], inc=(k == len(lst) - 1))

    def iota(o, pat, base, cm, fl=True):
        if fl:
            run("g", lambda: g.iota(o[0], pat, base, cm, allow_small_or_imprecise_dtypes=True), [], [o])
        else:
            run("g", lambda: g.iota(o[0], pat, base, cm), [], [o])

    def fill(o, n, val=0):
        iota(o, [[0, n]], val, 0)

    def dma(q, o, i):
        sem = "d%d" % nd[0]
        nd[0] += 1
        deps(q, [i[1]] if i[1] else [], [o[1]] if o[1] else [], (sem, 16))
        Q[q].dma_start(o[0], i[0]).then_inc(T.sem[sem], 16)

    def zl(name, r):
        return R(name, 15 - r, 143 - r)

    def tile(ps, z, buf, a=0, step=1):
        mms([(R(ps, 0, NB), zl(z, r), S(buf, a + step * r, NB, 16 * step)) for r in range(16)])

    def col(k):
        return R("C", k, k + 1)

    def lt(k):
        return R("LT", k, k + 1)

    def rm(k):
        return R("RM", k, k + 1)

    (cP, cR, cG, cT15, cW, cTQ, cAL, cU, cX, cY, cI0, cI1, cSB, cK, cP2, cP6, c2, cSW, cY0, cY1, cT0, cT1, cH, cN) = range(24)
    H2 = NN // 2
    CH = 384

    dma("s", R("X0", XP - 2, XP), (T.z[:, V - 2:V], None))
    dma("s", R("qi"), (T.q[:, :], None))
    for k in range(2):
        dma("y", R("X0", XP + NN * k, XP + NN * (k + 1)), (T.z[:, NN * k:NN * (k + 1)], None))
    dma("y", R("wb", 0, 1), (T.wt[:], None))

    iota(R("CI", 0, 1), [[1, 1]], 0, 1, fl=False)
    iota(R("J"), [[1, 144]], 0, 0)
    iota(R("JJ"), [[64, 8], [2, 16]], 0, 0)
    iota(R("J16"), [[16, 8], [0, 16]], 0, 0)
    iota(R("J8"), [[0, 16], [16, 8]], 0, 0)
    iota(R("JM"), [[16, 8], [0, 4], [1, 4]], 0, 0)
    iota(R("JC"), [[16, 8], [0, 2], [1, 8]], 0, 0)
    fill(R("K0"), NN)
    fill(S("WS", 1, NN, 2), NN)

    nbank = [0]

    def relu(out, a, n, x, pos, neg, step=1):
        ps = "pe%d" % (nbank[0] % 4)
        nbank[0] += 1
        mms([(R(ps, 0, n), R("IDN"), S(x, pos, n, 2)), (R(ps, 0, n), R("IDM"), S(x, neg, n, 2))])
        act(S(out, a, n, step), R(ps, 0, n), fn=F.Relu)

    def edge(x, par, j):
        c = XP + par + 2 * CH * j
        relu("EB%d" % par, c - XP + 15, CH + (1 if j == 3 and par == 0 else 0), x, c, c - 1, 2)

    def right(x, par, j):
        c = XP + par + 2 * CH * j
        relu("R2", CH * j, CH, x, c + 1, c)

    def span(x, par, j):
        c = XP + par + 2 * CH * j
        relu("R3", CH * j, CH, x, c + 1, c - 1)

    GB = ("pg", "pb")

    def term(buf, z, a, b, first=False, last=False, at=0, step=1):
        ps = GB[a // H2]
        mms(([(R(ps, 0, HB), R("IDN"), R("OF", 0, HB))] if first else [])
            + [(R(ps, 8 * (c % 6), 8 * (c % 6) + 8), S(buf, at + step * 128 * c, 128, step), R(z)) for c in range(a // 128, b // 128)],
            first, last)

    def terms(par, j, first=False):
        term("EB%d" % par, "ZWP", CH * j, CH * j + CH, first=first, at=15 + par, step=2)
        term("R2", "ZWP", CH * j, CH * j + CH)
        term("R3", "ZWN", CH * j, CH * j + CH)

    def ta(x, par, a, b):
        tt(R("TA", a, b), X(R(x, XP, XP + V), R("LA", a // 16, b // 16)), R("XC", a, b), A.min)

    def tb(x, par, a, b):
        tt(R("TB", a, b), X(R(x, XP, XP + V + 1), R("LA1", a // 16, b // 16)), R("XC", a, b), A.max)

    def own(q, x, par, j):
        o, i = R("XC", CH * j, CH * j + CH), S(x, XP + par + 2 * CH * j, CH, 2)
        if q == "v":
            cp(o, i)
        else:
            run("g", lambda: g.affine_select(o[0], i[0], [[0, CH]], A.is_ge, 0.0, 0, 0), [i], [o])

    def te(q, par, a, b):
        mv(q, R("TE", a, b), X(R("EB%d" % par, 16, 16 + V), R("LA", a // 16, b // 16)))

    def lists():
        cp(R("LA"), R("pa", 0, NB))
        ts(R("LA1"), R("pa", 0, NB), 1.0, A.add)

    def gathered(t, x, rest):
        par = t % 2
        ta(x, par, 0, H2)
        if t == 0:
            ts(R("ZWP"), R("J", 0, 128, 16), col(cG), A.is_equal, col(cW), A.mult)
            ts(R("ZWN"), R("ZWP"), -1.0, A.mult)
        tb(x, par, 0, H2)
        te("s", par, 0, H2)
        if t == 0:
            for fn, j in rest:
                fn(x, par, j)
        terms(par, 0, first=True)
        terms(par, 1)
        if t:
            for fn, j in rest:
                fn(x, par, j)
        term("TA", "ZWP", 0, H2)
        term("TB", "ZWN", 0, H2)
        term("TE", "ZWP", 0, H2, last=True)
        if t:
            ta(x, par, H2, NN)
        else:
            ms(R("WN3", 0, NN), 0.0)
        send(2 * t)
        if t == 0:
            ta(x, par, H2, NN)
        te("s", par, H2, NN - 256)
        te("s", par, NN - 256, NN)
        tb(x, par, H2, NN - 256)
        tb(x, par, NN - 256, NN)
        terms(par, 2, first=True)
        terms(par, 3)
        term("TA", "ZWP", H2, NN)
        term("TB", "ZWN", H2, NN - 256)
        term("TE", "ZWP", H2, NN - 256)
        term("TB", "ZWN", NN - 256, NN)
        term("TE", "ZWP", NN - 256, NN, last=True)
        send(2 * t + 1)

    hs = helpers(core, T, topo)

    def send(u):
        s = R("SND", u * HB, (u + 1) * HB)
        cp(s, R(GB[u % 2], 0, HB))
        deps("g", [s[1]], [], ("sent", 16 * (u + 1)))
        tr = []
        for k, c in enumerate([c for c, half, dests in hs if half == u % 2]):
            rid, pid = topo.addr(c, core)
            tr.append(RemoteDMATransfer(dst_ids=[DstId(rid=rid, pnc=pid)], dma_engine_mask=_bits(topo.engines(core, c)[8 * k:8 * k + 8]),
                                        remote_sem=T.sem["rx%d" % u], src=s[0], dst=T.RL[u // 2]))
        g.remote_dma_fused(tr, local_sem=T.sem.sent)

    def guests(par, n):
        act(X(R("WS", 0, V), R("LA", 0, n)), R("K0", 0, 16 * n), fn=F.Silu)
        act(R("ST"), S("WS", 1 - par, NN, 2))
        if n < NB:
            cp(X(R("WB"), R("LA", n, NB)), R("K1", 16 * n, NN))

    def moves(par, part):
        if part == 0:
            cp(R("KI"), R("LA"))
            ts(R("P1"), R("KI"), 1, A.logical_shift_right, 15, A.bitwise_and)
            ts(R("P2"), R("KI"), 5, A.logical_shift_right)
        else:
            ts(R("PA"), R("P1"), 288.0, A.mult, float(NB), A.add)
            tt(R("PB"), R("P2"), R("SB%d" % par), A.subtract)
            tt(R("DS"), R("PA"), R("PB"), A.add)

    def records(t):
        for j in range(4):
            ps, a = "pe%d" % j, CH * j
            lst = [(R(ps, 0, CH), R("RS"), R("K1", a, a + CH))]
            if t == 0:
                lst += [(S(ps, r // 2, HB, 8), R("RQ0" if r % 2 else "RC0", rows=16),
                         R("KQ", 192 * r + HB * j, 192 * r + HB * j + HB, rows=16)) for r in range(16)]
            else:
                lst += [(R(ps, 0, CH), R("RC"), R("QC", a, a + CH))]
            mms(lst, last=False)

    def targets(t, h):
        par = t % 2
        for j in (2 * h, 2 * h + 1):
            mms([(R("pe%d" % j, 0, CH), R("RQ"), R("QO", CH * j + par, CH * j + CH + par))], False, False)
        if par and h == 0:
            mms([(R("pa", 0, 1), R("RQ"), R("QO", 0, 1))])
            cp(R("T2", 15, 16), R("pa", 0, 1))

    def keep(q, buf, j, bias):
        rl(q, R(buf, 16 + CH * j, 16 + CH * j + CH), R("pe%d" % j, 0, CH), col(bias))

    def fetch(u):
        wait("y", "rx%d" % u, 2 * len(T.cores))
        dma("y", R("RXS", CH * (u % 2), CH * (u % 2) + CH), (T["RX%d" % u][:], None))

    def arrive(t, h):
        par, ps, a = t % 2, ("pg", "pc")[h], CH * h
        for k0, k1 in ((0, 1), (1, 4)):
            cp(R("RXF", a + NB * k0, a + NB * k1), R("RXS", a + NB * k0, a + NB * k1))
            mms([(S(ps, k, 16, 4, NB), R("RXF", a + NB * k, a + NB * k + NB), R("RM")) for k in range(k0, k1)], k0 == 0, k1 == 4)
        if h:
            if t:
                targets(t, 1)
            keep("v", "Y", 0, cY0 + par)
            cp(R("LI"), R("pb", 0, NB))
        else:
            moves(par, 0)
        mc = R("mc", 64 * h, 64 * h + 64, rows=NB)
        ts(mc, R(ps, 0, 64, rows=NB), float(8 * OFF), A.is_gt)
        for j in range(2):
            mms([(S("pe%d" % (2 * h + j), 128 * (c % 3) + e, 64, 2), R("E12", 128 * (6 * e + c), 128 * (6 * e + c) + 128, rows=NB), mc)
                 for c in range(3 * j, 3 * j + 3) for e in range(2)], first=False)
        keep("s", "Y", 1 + h, cY0 + par)
        if h:
            moves(par, 1)
            keep("v", "Y", 3, cY0 + par)

    def decide(t):
        par = t % 2
        fetch(2 * t)
        fetch(2 * t + 1)
        if t:
            mms([(R("pb", 0, NB), zl("ZQ", r), S("WB", 1 - par + 2 * r, NB, 32)) for r in range(16)], last=False)
            targets(t, 0)
            arrive(t, 0)
        mms([(R("pb", 0, NB), zl("ZQ", r), S("ST", r, NB, 16)) for r in range(16)], first=(t == 0))
        if t == 0:
            arrive(t, 0)
        arrive(t, 1)
        tile("pa", "ZG", "Y", 16)
        for k in range(4):
            mv("sv"[k % 2], R("T3", CH * k, CH * k + CH), X(R("Y"), R("LI", QB * k, QB * k + QB)))
        for h in range(2):
            mms([(R("pb", HB * h, HB * h + HB), zl("ZG", r), S("T3", H2 * h + r, HB, 16)) for r in range(16)], h == 0, h == 1)
        cp(R("mn"), R("pa", 0, NB))
        for j in range(4):
            keep("s" if j else "v", "T2", j, cT0 + par)
        if par:
            rl("s", R("W", 16 + V, 17 + V), R("pe3", CH - 1, CH), col(cT0 + par))
        tt(R("S2"), R("mn"), R("DS"), A.mult)
        tt(R("dd"), R("pb", 0, NB), R("mn"), A.subtract)
        mms([(R("pc", 0, NB), R("TLT"), R("dd")), (R("pc", 1, NB), R("TGE"), R("dd", 0, NB - 1))]
            + ([] if par else [(R("pc", 0, NB), R("IDM"), R("mn")), (R("pc", 1, NB), R("IDN"), R("mn", 0, NB - 1))]))
        tt(R("S2"), R("S2"), R("SB%d" % par), A.add)
        scan(R("base"), R("pc", 0, NB), R("C32"), col(cI0 + par), A.add, A.add)
        cp(R("LS"), R("S2"))
        cp(R("LB"), R("base"))
        tt(X(R("W", 16, 16 + V), R("LB")), R("T3"), R("T2", 16 - par, 16 - par + NN), A.add)
        if t < RO - 1:
            act(R("hb", 0, NB), R("base"), bias=col(cH), fn=F.Relu)
            mms([(R("pa", 0, NB), R("IDF"), R("base")), (R("pa", 0, NB), R("IDM"), R("hb", 0, NB))])
            for k in (1, 2):
                act(R("hb", k * NB, k * NB + NB), R("hb", 0, NB))
            dma("y", row("WN3", 0, 0, 3 * NN), R("hb"))
            for k, d in enumerate((0.0, 1.0, -1.0)):
                act(R("lo", k * NB, k * NB + NB), R("pa", 0, NB), bias=d)
            dma("s", row("WN3", 1, 0, 3 * NN), R("lo"))
            if t == 0:
                odd_round()
            w3, w2 = "WN3", "WN2"
        else:
            for k, d in enumerate((0.0, 1.0, -1.0)):
                act(R("b3", k * NB, k * NB + NB), R("base"), bias=d)
            dma("s", row("WS", 0, 0, 3 * NN), R("b3"))
            w3, w2 = "WS", "WF2"
        act(S(w2, par, NN, 2), X(R(w3), R("LS")))
        OS = 64
        act(S(w2, 1 - par, 16 * OS, 2), X(R(w3), R("LSO", 0, OS)))
        cp(S(w2, 1 - par + 32 * OS, NN - 16 * OS, 2), X(R(w3), R("LSO", OS, NB)))

        def w(s):
            return S("W", 16 + s, NB, 32)

        def pw(a, b):
            return R("pg", a, b, rows=NB)

        mms([(pw(0, 512), R("ZR"), R("K1", 0, 512))], last=False)
        mms([(pw(16 * s - 16, 16 * s + 32), w(s), R("SELW")) for s in range(1, 31)]
            + [(pw(0, 32), w(0), R("SELW", 16, 48)), (pw(480, 512), w(31), R("SELW", 0, 32)),
               (pw(496, 512), w(32), R("SELW", 0, 16)), (pw(0, 16), w(-1), R("SELW", 32, 48))], first=False)
        for k in range(8):
            cp(R("TW", 64 * k, 64 * k + 64, rows=NB), S("pg", k, 64, 8, NB))

    def turn(ps, a, par, f):
        mms([(R(ps, a, a + NB), S("TW", 2 * par + f, 128, 4, NB), R("IDF", 0, NB, rows=NB))])

    ts(R("CI", 1, 2), R("CI", 0, 1), 15, A.bitwise_and)
    cp(col(cP), R("CI", 0, 1))
    cp(col(cR), R("CI", 1, 2))
    for k in range(12):
        act(S("EB0", 16 + 256 * k, 128, 2), R("J", 0, 128), scale=0.0, bias=-200.0)
    tt(col(cG), col(cP), col(cR), A.subtract)
    ts(col(cK), col(cR), float(NB), A.mult)
    ts(R("IDN"), R("J", 0, 128), col(cP), A.is_equal)
    ts(col(cTQ), col(cG), 4.0, A.mult, col(cR), A.add)
    ts(R("IDM"), R("J", 0, 128), col(cP), A.is_equal, -1.0, A.mult)
    ts(R("KI"), R("J", 0, NB), col(cK), A.add)
    for k in range(2):
        ts(R("SEL", 128 * k, 128 * k + 128), R("JJ"), col(cTQ), A.subtract, float(16 * k), A.is_equal)
    ts(R("P2"), R("KI"), 63, A.bitwise_and)
    ts(R("P1"), R("KI"), 4032, A.bitwise_and)
    ts(col(cT15), col(cG), 15.0, A.add)
    ts(R("KB", NB, 2 * NB), R("P2"), 16.0, A.add)
    cp(R("KB", 0, NB), R("P1"))
    ms(col(cH), -12.0)
    cp(R("qf"), R("qi"))
    mms([(R("pa", 0, NB), R("SEL", 128 * k, 128 * k + 128), S("qf", k, NB, 2)) for k in range(2)])
    act(R("qh", 0, 192), R("qf"), bias=col(cH), fn=F.Relu)
    ms(R("OF"), float(OFF))
    ts(R("LT", 0, 17), R("J", 0, 17), col(cR), A.is_gt)
    ts(R("RM"), R("J", 0, 16), col(cR), A.is_equal)
    ts(R("ZQ"), R("J"), col(cT15), A.is_equal, lt(2), A.mult)
    lists()
    tt(R("qh", 192, 384), R("qf"), R("qh", 0, 192), A.subtract)
    for k in range(2):
        dma("y", row("K0", k), R("KB", k * NB, k * NB + NB))
    for f in range(2):
        dma("y", (T.KQ[8 * f:8 * f + 8, :], ("KQ", 0, V, ("row", f))), R("qh", 192 * f, 192 * f + 192))

    def matrices():
        ts(R("B8"), R("J8"), col(cG), A.is_equal)
        ts(col(cU), lt(12), lt(8), A.subtract, lt(4), A.subtract)
        ts(R("CI", 3, 4), R("CI", 0, 1), 120, A.bitwise_and)
        ts(col(cAL), col(cU), BIG, A.mult, rm(14), A.add)
        cp(col(cX), R("CI", 3, 4))
        ts(R("DA"), R("J", 0, 128), col(cP), A.is_equal, col(cAL), A.mult)
        ts(R("RM8", 0, 12), R("J", 0, 96, 8), col(cX), A.is_equal)
        ts(col(c2), lt(2), 2.0, A.mult)
        ts(col(cP2), col(cP), 2.0, A.add)
        ts(col(cP6), col(cP), 6.0, A.add)
        ts(R("RS"), R("JM"), col(cP), A.is_equal, col(c2), A.mult)
        ts(R("RC"), R("JC"), col(cP2), A.is_equal, lt(2), A.mult)
        ts(R("RQ"), R("J", 0, 128), col(cP6), A.is_equal, lt(2), A.mult)

    def matrices2():
        ts(R("ZG"), R("J"), col(cT15), A.is_equal, rm(14), A.mult)
        ts(R("BLK"), R("J16"), col(cG), A.is_equal)
        ts(R("DA"), R("J", 0, 128), col(cP), A.is_gt)
        ts(R("IDF"), R("J", 0, 128), col(cP), A.is_equal)
        tt(R("TLT"), R("DA"), R("BLK"), A.mult)
        ts(R("CI", 4, 5), R("CI", 0, 1), 14, A.bitwise_and)
        ts(col(cU), lt(12), lt(8), A.subtract, rm(14), A.add)
        tt(R("TGE"), R("BLK"), R("TLT"), A.subtract)
        ts(col(cSW), R("CI", 4, 5), 4.0, A.mult)
        ts(col(cY), col(cU), -1.0, A.add, 65536.0, A.mult)
        ts(col(cX), col(cG), 0.0625, A.mult, col(cSW), A.add)
        ts(col(cU), lt(12), lt(8), A.subtract, -BIG, A.mult)
        ts(col(cN), lt(8), -1.0, A.add, 65536.0, A.mult)
        ts(R("SELW"), R("J", 0, 48), col(cX), A.is_equal)
        ts(col(cY), col(cY), col(cU), A.add)
        ts(col(cN), rm(5), col(cN), A.add)
        tt(col(cU), rm(1), rm(5), A.add)
        ts(col(cSB), col(cR), 288.0, A.mult)
        ts(col(cY0), rm(9), -32.0, A.mult, col(cY), A.add)
        ts(col(cT0), col(cU), -32.0, A.mult, col(cN), A.add)
        ts(col(cI0), col(cR), 2.0, A.mult, -31.0, A.add)
        ts(R("SB0"), R("J", 0, NB), col(cSB), A.add, 192.0, A.add)
        ts(R("LSO"), R("J", 0, NB), col(cSB), A.add)
        ms(R("C32"), 32.0)
        ms(R("ZR"), 0.0)
        ms(R("Y", 0, 16), 0.0)

    def odd_round():
        act(col(cX), rm(0), scale=3008.0)
        act(col(cY), rm(15), scale=float(1 - 288 * 16), bias=col(cSB))
        act(col(cY1), rm(9), bias=col(cY0))
        act(col(cN), rm(1), scale=63.0, bias=col(cX))
        act(col(cK), col(cY), bias=480.0)
        act(col(cT1), col(cU), bias=col(cT0))
        act(R("WN3", 3 * NN, 3 * NN + 16), R("C32", 0, 16), scale=0.0, bias=col(cN))
        act(R("SB1"), R("J", 0, NB), bias=col(cK))
        act(col(cI1), col(cI0), bias=-1.0)
        act(col(cX), rm(15), scale=float(3 * NN - 288), bias=R("SB1", NB - 1, NB))
        act(R("QO", NN, NN + 16), R("C32", 0, 16), scale=0.0)
        act(R("SB1", NB - 1, NB), col(cX))

    matrices()
    for j in range(4):
        own("v", "X0", 0, j)
        if j == 0:
            cp(R("X0", XP + V, XP + V + 1), R("X0", XP, XP + 1))
        edge("X0", 0, j)
        if j < 2:
            right("X0", 0, j)
            span("X0", 0, j)
    cp(col(cW), R("wb", 0, 1))
    gathered(0, "X0", [(right, 2), (span, 2), (right, 3), (span, 3)])
    fill(R("W"), XW)
    fill(R("WN3", NN, 3 * NN), V)
    fill(S("EB1", 17, NN, 2), NN, -200)
    guests(0, NB)
    cp(R("K1"), R("K0"))
    ts(R("CI", 5, 6), R("CI", 0, 1), 7, A.bitwise_and)
    ts(R("CI", 6, 7), R("CI", 0, 1), 3, A.logical_shift_right)
    ts(col(cU), R("CI", 5, 6), 16.0, A.mult, 2.0, A.add)
    ts(col(cX), R("CI", 6, 7), col(cU), A.add)
    ts(R("RC0"), R("JC"), col(cX), A.is_equal)
    ts(R("RQ0"), R("J", 0, 128), col(cX), A.subtract, 4.0, A.is_equal)
    mms([(R("pc", 0, 128), R("B8"), R("DA"))])
    for r in range(12):
        ts(R("E12", 128 * r, 128 * r + 128), R("pc", 0, 128), R("RM8", r, r + 1), A.mult)
    records(0)
    matrices2()

    for t in range(RO):
        xo, xn = "X%d" % (t % 2), "X%d" % ((t + 1) % 2)
        par = (t + 1) % 2
        win = R(xo, XP, XP + V)
        decide(t)
        if t < RO - 1:
            fill(S("WS", 1 - par, NN, 2), NN)
            fill(S("WB", 1 - par, NN, 2), NN)
            turn("pa", 0, par, 1)
            turn("pb", 0, 1 - par, 0)
            turn("pc", 0, par, 0)
            turn("pg", 0, 1 - par, 1)
            cp(R("LQ", 0, NB), R("pa", 0, NB))
            cp(R("LX", 0, NB), R("pb", 0, NB))
            act(R("QC"), X(R("WN2"), R("LQ", 0, NB)))

            def others(a, b):
                cp(S(xn, XP + 1 - par + 32 * a, 16 * (b - a), 2), X(win, R("LX", a, b)))

            def cands(a, b):
                cp(S(xn, XP + par + 32 * a, 16 * (b - a), 2), X(win, R("LX", NB + a, NB + b)))
                for j in range(a // QB, b // QB):
                    own("g", xn, par, j)

            def wrap():
                cp(R(xn, XP + V, XP + V + 1), R(xn, XP, XP + 1))

            if par == 0:
                cp(R(xn, 0, XP), X(win, R("LX", NB - 2, NB)))
            others(0, HB + 2 * par)
            cp(R("LX", NB, 2 * NB), R("pc", 0, NB))
            cp(R("LQ", NB, 2 * NB), R("pg", 0, NB))
            span(xn, par, 0)
            span(xn, par, 1)
            cands(0, QB)
            wrap()
            edge(xn, par, 0)
            right(xn, par, 0)
            cands(QB, HB)
            tile("pa", "ZQ", "QC")
            edge(xn, par, 1)
            right(xn, par, 1)
            others(HB + 2 * par, NB)
            span(xn, par, 2)
            span(xn, par, 3)
            cands(HB, NB)
            lists()
            edge(xn, par, 2)
            edge(xn, par, 3)
            gathered(t + 1, xn, [(right, 2), (right, 3)])
            fill(R("W"), XW)
            if t == 0:
                fill(R("WS", V, 3 * NN), NN)
            guests(par, 60)
            for q, a, b in (("v", 0, HB + 2), ("s", HB + 2, NB)):
                mv(q, R("QO", 16 * a, 16 * b), X(R("WN2"), R("LQ", NB + a, NB + b)))
            records(t + 1)
        else:
            turn("pa", 0, 1, 0)
            turn("pb", 0, 0, 0)
            turn("pc", 0, 0, 1)
            turn("pc", NB, 1, 1)
            cp(R("LX", NB, 2 * NB), R("pa", 0, NB))
            cp(R("LX", 0, NB), R("pb", 0, NB))
            for j in range(4):
                if j == 1:
                    cp(R("LQ"), R("pc", 0, 2 * NB))
                for e, q in enumerate("vs"):
                    mv(q, S(xn, XP + e + 2 * CH * j, CH, 2), X(win, R("LX", NB * e + 24 * j, NB * e + 24 * j + 24)))
                dma("y", (T.yz[:, 2 * CH * j:2 * CH * (j + 1)], None), R(xn, XP + 2 * CH * j, XP + 2 * CH * (j + 1)))
            for j in range(2):
                for e, q in enumerate("vs"):
                    mv(q, S("QF", e + NN * j, H2, 2), X(R("WF2"), R("LQ", NB * e + HB * j, NB * e + HB * j + HB)))
                dma("y", (T.yq[:, NN * j:NN * (j + 1)], None), row("QF", 0, NN * j, NN * (j + 1)))

    for k in range(nd[0]):
        wait("y", "d%d" % k, 16)
    for q in cnt:
        wait("y", "q" + q, cnt[q])
    g.wait_ge(T.sem.sent, 32 * RO)
